import numpy as np, ml_dtypes
CORES = [23,119,17,113]
N = 4
BF = ml_dtypes.bfloat16
def gentries(a):
    return np.ascontiguousarray(a.reshape(8, 16, -1).transpose(0, 2, 1)).reshape(8, -1)
def gtable(e):
    e = np.asarray(e); return np.ascontiguousarray(e.reshape(8, -1, 16).transpose(0, 2, 1)).reshape(128, -1).astype(np.int32)
P, LG, I, K, M, RO = 4096, 12, 256, 32, 16, 3
RHO, KA, KB, LIGHT, HALF = 72, 7, 8, 24, 7168
def lists(rng):
    return np.argsort(rng.random((N, 8, 4, P)), axis=-1)
def parts(rng):
    x = rng.integers(0, 256, (N, 8, 16, P)); z = rng.integers(0, 256, (N, 8, 16, 4 * I))
    lev = rng.permuted(np.tile(np.array([0.95, 0.83, 0.74, 0.69, 0.65, 0.6, 0.53, 0.42]), (N, 1)), axis=1)
    w = np.minimum(rng.geometric(lev[:, :, None], (N, 8, P)), 8)
    return x, w, z, lists(rng)
def pack(x, w, z, mem):
    return {"pt": np.ascontiguousarray(x.reshape(N, 128, P)).astype(np.float32).astype(BF), "w0": np.ascontiguousarray(w).astype(np.float32).astype(BF),
            "z0": np.ascontiguousarray(z.reshape(N, 128, 4 * I)).astype(np.float32).astype(BF), "lm": np.stack([gtable(a.reshape(8, -1)) for a in mem])}
def total(rng, s):
    e = (s - P) >> 4; w = np.ones(P, np.int64); w[:e] = 8; w[e:e + s - P - 7 * e] = 2
    return rng.permutation(w)
def setup_inputs(rng):
    return pack(*parts(rng))
def setup_inputs_spread(rng):
    def uneven(n):
        v = np.floor(np.exp2(8 * rng.random((N, 8, 1, n))) * rng.random((N, 8, 16, n))).astype(np.int64)
        return np.where(rng.random(v.shape) < 0.5, v, 255 - v)
    x, z = uneven(P), uneven(4 * I)
    ex = rng.permuted(np.tile(np.array([1.0, 2.0, 3.0, 5.0, 8.0, 12.0, 16.0, 24.0]), (N, 1)), axis=1)
    w = 1 + np.minimum(np.floor(8 * rng.random((N, 8, P)) ** ex[:, :, None]).astype(np.int64), 7)
    return pack(x, w, z, lists(rng))
def setup_inputs_ends(rng):
    def two(n):
        e = 255 * rng.integers(0, 2, (N, 8, 16, n)); m = rng.integers(0, 7, (N, 8, 1, n))
        return np.where(m == 0, 0, np.where(m == 1, 255, e))
    x, z = two(P), two(4 * I); w = np.ones((N, 8, P), np.int64)
    s = rng.permuted(np.tile(np.array([0.02, 0.06, 0.1, 0.15, 0.3, 0.5]), (N, 1)), axis=1)
    w[:, 1:7] = np.where(rng.random((N, 6, P)) < s[:, :, None], 8, 1); w[:, 1:7, 0] = 8; w[:, 1:7, P - 1] = 8
    w[0::2, 0] = 8; w[1::2, 7] = 8
    z[:, 1:6:2, :, I - 1::I] = 255; z[:, 0:7:2, :, I - 1::I] = 0
    for r in (0, N - 1): x[r, 7] = 255 * (rng.random((16, P)) < 0.03125)
    z[0, 7] = 255; z[1, 7] = 255
    inner = np.arange(4 * I) % I < I - 1; coin = rng.random((2, 4 * I)) < 0.5
    z[0:2, 7, 7] = np.where(inner & coin, 254, 255); z[0:2, 7, 15] = np.where(inner & ~coin, 254, 255)
    h = np.arange(P >> 1); seq = np.stack([h, P - 1 - h], axis=1).reshape(I, M)
    lan = np.argsort(rng.random((N, 4, 4, I)), axis=-1)
    lan[:, :, 0] = np.concatenate([1 + np.argsort(rng.random((N, 4, I - 1)), axis=-1), np.zeros((N, 4, 1), np.int64)], axis=-1)
    mem = lists(rng); mem[:, 0::2] = seq[lan].reshape(N, 4, 4, P)
    return pack(x, w, z, mem)
def setup_inputs_corners(rng):
    x, w, z, mem = parts(rng); o = [int(a) for a in rng.permutation(8)]
    x[:, o[0]] = rng.integers(100, 101 + (RHO >> 1), (N, 16, P)); z[:, o[0]] = rng.integers(100, 101 + (RHO >> 1), (N, 16, 4 * I))
    b = rng.integers(110, 141, (1, 16, 1)); x[:, o[1]] = b
    n = rng.choice(np.array([11, 12, 13, 16]), (N, 1, 4 * I)); pl = np.argsort(rng.random((N, 16, 4 * I)), axis=1)
    z[:, o[1]] = b + np.where(pl < n, RHO, RHO + 1) * rng.choice(np.array([-1, 1]), (N, 16, 4 * I))
    x[:, o[2]] = rng.integers(200, 256, (N, 16, P)); z[:, o[2]] = rng.integers(0, 21, (N, 16, 4 * I))
    for r in range(N):
        w[r, o[0]] = total(rng, (HALF, HALF + 1, 2 * P, 2 * P - 1)[r % 4]); w[r, o[3]] = total(rng, (2 * P + 1, 2 * P, 2 * P - 1, P)[r % 4])
        k = rng.integers(0, 4, (I, 1)); k[:4, 0] = rng.permutation(4); k[I - 1, 0] = 1 + r % 2
        twos = np.where(k == 0, 0, np.where(k == 1, (M >> 1) - 1, M >> 1))
        v = np.where(k == 3, 8, np.where(np.arange(M)[None, :] < twos, 2, 1))
        w[r, o[2], mem[r, o[2], 0]] = v.reshape(-1)
    w[:, o[4]] = 8; w[:, o[5]] = 1; w[:, o[6]] = 1; w[:, o[6], :P >> 2] = 8
    m = rng.integers(0, 3, (N, 1, 4 * I)); z[:, o[7]] = np.where(m == 0, 0, np.where(m == 1, 255, z[:, o[7]]))
    return pack(x, w, z, mem)
def setup_inputs_crowd(rng):
    x, w, z, mem = parts(rng); o = [int(a) for a in rng.permutation(8)]
    j = o.index(7 - o[0]); o[j], o[7] = o[7], o[j]
    for g in o[:5]:
        x[:, g] = rng.integers(200, 256, (N, 16, P)); z[:, g] = rng.integers(0, 21, (N, 16, 4 * I))
    w[:, o[0]] = rng.integers(2, 9, (N, P)); w[:, o[1]] = rng.integers(2, 9, (N, P)); w[:, o[2]] = 1; w[:, o[3]] = 1
    for r in range(N):
        a = int(rng.integers(0, I)); a = I - 1 if r == 0 else 0 if r == 1 else a
        z[r, o[1], :, a::I] = 227
        a = int(rng.integers(0, I)); a = I - 1 if r == N - 1 else a
        w[r, o[3], mem[r, o[3], 0, a * M:(a + 1) * M]] = 8
    mem[:, o[4], 1] = mem[:, o[4], 0].reshape(N, -1, 2, M)[:, :, ::-1].reshape(N, P)
    z[:, o[4], :, 1:I:2] = 227; w[:, o[4]] = np.minimum(rng.geometric(0.9, (N, P)), 8)
    z[:, o[5]] = 0
    x[:, o[6]] = rng.integers(200, 256, (N, 16, P)); z[:, o[6]] = 227; w[:, o[6]] = 1
    for r in range(N):
        n = int(rng.integers(7 * I >> 4, (17 * I >> 5) + 1)); a = rng.permutation(I)[:n]
        zv = z[(r + 1) % N, o[6]]; zv[:, a] = rng.integers(0, 21, (16, n))
        wv = w[r, o[6]]; wv[mem[r, o[6], 0].reshape(I, M)[a, :M >> 4]] = 8
    x[:, o[7]] = rng.integers(200, 256, (N, 16, P)); z[:, o[7]] = rng.integers(0, 21, (N, 16, 4 * I)); w[:, o[7]] = rng.integers(2, 9, (N, P))
    z[:, o[7], :, :I] = 227; z[:, o[7], :, 2 * I:3 * I] = 227
    for r in range(1, N, 2):
        a = int(rng.integers(0, I)); a = I - 1 if r == N - 1 else 0 if r == 1 else a
        z[r, o[7], :, I + a] = 227
    return pack(x, w, z, mem)
def check_inputs(d):
    bad = []
    for k, lo, hi in (("pt", 0, 255), ("w0", 1, 8), ("z0", 0, 255), ("lm", 0, P - 1)):
        a = np.asarray(d[k]).astype(np.float64)
        if not np.all((a >= lo) & (a <= hi)): bad.append("range of " + k)
        if np.any(a != np.floor(a)): bad.append("whole numbers of " + k)
    e = np.sort(np.stack([gentries(a) for a in np.asarray(d["lm"])]).reshape(-1, P), axis=1)
    if np.any(e != np.arange(P)[None, :]): bad.append("lm: the members of a class are all different")
    return bad
def reference(pt, w0, z0, lm):
    x = pt.astype(np.float32).astype(np.int64).reshape(N, 8, 16, P); w = w0.astype(np.float32).astype(np.int64).reshape(N, 8, P)
    z = z0.astype(np.float32).astype(np.int64).reshape(N, 8, 16, 4 * I); mem = np.stack([gentries(a) for a in lm]).astype(np.int64).reshape(N, 8, 4, I, M)
    kap = KA + KB * np.arange(K); cof = 2 * np.arange(16) + 1
    A = np.zeros((N, 8), np.int64); tally = np.zeros((N, 8, RO), np.int64)
    for t in range(RO):
        c = (t % 4, (t + 1) % 4); zn = z.copy()
        for r in range(N):
            q = (r + 1 + t % (N - 1)) % N
            for g in range(8):
                zz = [z[q, g, :, a * I:(a + 1) * I] for a in c]
                wg = w[r, g].copy(); T = min(int(np.sum(wg)), 2 * P); E = np.repeat(np.arange(P), wg)[:T]
                u = np.dot(cof, zz[0])
                h = (((u[:, None] * kap[None, :]) >> 4) + 61 * np.arange(I)[:, None] + A[r, g]) & (P - 1)
                net = E[(h * (T >> 1)) >> (LG - 1)]
                p = x[r, g][:, net]
                miss = [~np.any(np.sum(np.abs(p - b[:, :, None]) <= RHO, axis=0) >= 12, axis=1) for b in zz]
                y = (np.max(p, axis=2) + np.min(p, axis=2)) >> 1
                mark = np.zeros(P, bool); heavy = 0
                for m in (0, 1):
                    sel = miss[0] if m == 0 else miss[1] & ~miss[0]
                    s = np.sum(wg[mem[r, g, c[m]]], axis=1); light = sel & (s < LIGHT)
                    mark[mem[r, g, c[m]][light]] = True; heavy = heavy + int(np.sum(sel & ~light))
                    zn[q, g, :, c[m] * I:(c[m] + 1) * I] = np.where(sel[None, :], (zz[m] + y) >> 1, zz[m])
                wg = np.where(mark, np.minimum(2 * wg, 8), wg)
                if int(np.sum(wg)) > HALF: wg = (wg + 1) >> 1
                w[r, g] = wg; A[r, g] = heavy; tally[r, g, t] = heavy
        z = zn
    return {"yw": w.astype(np.float32), "yz": z.reshape(N, 128, 4 * I).astype(np.float32).astype(BF), "ya": tally.astype(np.float32)}

@@ -1,0 +1,516 @@
+from concourse.mybir import AluOpType, AxisListType, ActivationFunctionType
+
+OP = AluOpType
+AF = ActivationFunctionType
+ALPHA = 226.0 / 32768.0
+
+PIECES = {("setup", 0): [(0, 0), (0, 1), (0, 2), (0, 3)], (2, 0): [(1, 0)], (4, 0): [(1, 1)], (5, 0): [(1, 2)], (6, 0): [(1, 3)],
+          ("marks", 0): [(2, 0), (2, 1), (2, 2)], (3, 1): [(2, 3)],
+          ("marks", 1): [(3, 0), (3, 1), (3, 2)], (3, 2): [(3, 3)]}
+WRAP = {0: [1, 15], 1: [15], 2: [15]}
+LATE = 14
+VUNITS = {0: [0, 2, 3, 4, 6, 7, 8, 10, 11, 12, 14, 15], 1: [4, 8, 12], 2: [4, 8, 12]}
+NETQ = ["VVVV", "VSVS", "VSVS"]
+MEMBERS = {("pre", 0): [0], (9, 0): [1], ("pre", 1): [0, 1], ("pre", 2): [0, 1]}
+SCANS = {2: (0, 0), 4: (0, 1), 8: (1, 0), 10: (1, 1)}
+DV = 2
+LAG = 3
+
+
+def _table():
+    out = {"ps": ("psum", [128, 4096], "float32")}
+    for d, cols in (("bfloat16", "w0r:4096 ptx:4112 dif:4096 win:12288 ex:8192 net:8192 tmx:4096 tmn:4096 kmx:2048 kmn:2048 ab:4096 ind:6144"
+                     " nat:4096 rbf:4096 zo:1024 zin:1024 zrr:512 fin:1024 znew:1536 edg:2048 xpd:2048 idm:128 nid:128 aid:128 nad:128 bo:128"
+                     " lt:128 tri:128 tru:128 b8:16 b2:128 uhi:128 ulo:128 u128:128 wr:272 wf:256 wt:256 w1:256 w2:256 zx0:512 zx1:512"
+                     " h01:1024 hts:512 sel:512 m1:256 lg:512 lfl:512 mx0:256 mn0:256 mxx:256 mnn:256 zd:512 zm:512"),
+                    ("float32", "invw:4096 vals:4096 colb:16 pbc:16 cf:512 ca:512 lim:256 st:256 sm:16 t2:16 hv:16 sc:16 bi:16 acc:16 yat:16 a16:16"),
+                    ("int32", "ip:128 ij:128 pg:128 pb:128 jg:128 jb:128 dw:128 ci1:128 ci2:128 ci3:128 ci4:128 j16:256 si:16 hx:512 hy:512"
+                     " yy:256 zs:512 zh:512 ivi:256"),
+                    ("uint16", "lmu:1024 inv:1024 stu:256 hu:512")):
+        for c in cols.split():
+            n, w = c.split(":")
+            out[n] = ("sbuf", [128, int(w)], d)
+    return out
+
+
+SCRATCH = _table()
+INTS = [n for n in SCRATCH if SCRATCH[n][2] == "int32"]
+NDMA = 16
+SEMAPHORES = (["qv", "qs", "qp", "qg", "sent", "az01", "az2", "az3", "ar1", "ar2", "af0", "af1", "af2", "af3"]
+              + ["d%d" % k for k in range(NDMA)])
+QSEM = {"V": "qv", "S": "qs", "P": "qp", "G": "qg"}
+
+
+def rank_program(g, core, T, topo):
+    rank = T.rank_of(core)
+    if rank is None:
+        return
+    eng = {"V": g.vector, "S": g.scalar, "P": g.tensor, "G": g, "Y": g.sync}
+    known = {q: {} for q in eng}
+    count = {q: 0 for q in eng}
+    recs, banks, totals, ndma = {}, {}, {}, [0]
+    ps = T.ps
+
+    def wait(q, toks):
+        for s, v, ck in sorted(toks, key=lambda k: -sum(k[2].values())):
+            if known[q].get(s, 0) < v:
+                eng[q].wait_ge(T.sem[s], v)
+            for s2, v2 in ck.items():
+                if known[q].get(s2, 0) < v2:
+                    known[q][s2] = v2
+
+    def deps(q, R, W, B):
+        toks = []
+        for n, lo, hi in R:
+            toks += [r[3] for r in recs.get(n, []) if r[2] == "w" and r[0] < hi and lo < r[1]]
+        for n, lo, hi in W:
+            toks += [r[3] for r in recs.get(n, []) if r[0] < hi and lo < r[1]]
+        for b in B:
+            toks += [tk for q2, tk in banks.get(b, {}).items() if q2 != q]
+        return toks
+
+    def note(q, tok, R, W, B):
+        for n, lo, hi in W:
+            recs[n] = [r for r in recs.get(n, []) if not (lo <= r[0] and r[1] <= hi)] + [(lo, hi, "w", tok, q)]
+        for n, lo, hi in R:
+            recs[n] = [r for r in recs.get(n, []) if not (r[2] == "r" and r[4] == q and lo <= r[0] and r[1] <= hi)] + [(lo, hi, "r", tok, q)]
+        for b in B:
+            banks.setdefault(b, {})
+            banks[b][q] = tok
+
+    def token(q, s, v):
+        ck = dict(known[q])
+        ck[s] = v
+        totals[s] = v
+        return (s, v, ck)
+
+    def op(q, fn, R=(), W=(), B=()):
+        wait(q, deps(q, R, W, B))
+        count[q] += 1
+        fn(eng[q]).then_inc(T.sem[QSEM[q]], 1)
+        note(q, token(q, QSEM[q], count[q]), R, W, B)
+
+    def group(bank, mats):
+        for k, (o, l, r, a, b, R) in enumerate(mats):
+            wait("P", deps("P", R, (), (bank,) if k == 0 else ()))
+        for o, l, r, a, b, R in mats:
+            ins = g.tensor.matmul(o, l, r, a, b)
+        count["P"] += 1
+        ins.then_inc(T.sem.qp, 1)
+        tok = token("P", "qp", count["P"])
+        for o, l, r, a, b, R in mats:
+            note("P", tok, R, (), (bank,))
+
+    def dma(q, out, in_, R=(), W=()):
+        wait(q, deps(q, R, W, ()))
+        s = "d%d" % ndma[0]
+        ndma[0] += 1
+        eng[q].dma_start(out, in_).then_inc(T.sem[s], 16)
+        note(q, token(q, s, 16), R, W, ())
+
+    def send(to, out, in_, sem, R):
+        dst = T.cores[to % len(T.cores)]
+        wait("G", deps("G", R, (), ()))
+        rid, pid = topo.addr(dst)[:2]
+        m = 0
+        for e in topo.engines(core, dst)[:8]:
+            m |= 1 << e
+        g.remote_dma(out, in_, T.sem[sem], T.sem.sent, pid, rid, m)
+        totals["sent"] = totals.get("sent", 0) + bin(m).count("1")
+
+    def arrive(sem, frm, name, lo, hi):
+        n = len(topo.engines(T.cores[frm % len(T.cores)], core)[:8])
+        totals[sem] = n
+        recs.setdefault(name, []).append((lo, hi, "w", (sem, n, {sem: n}), "net"))
+
+    def full(n):
+        return (n, 0, SCRATCH[n][1][1])
+
+    def half(n, k, w=256):
+        return (n, k * w, k * w + w)
+
+    def sq(n, b=0):
+        return (n, b * 128, b * 128 + 128)
+
+    def ap(x):
+        n, lo, hi = x[0], x[1], x[2]
+        return T[n][:, lo:hi:x[3]] if len(x) > 3 else T[n][:, lo:hi]
+
+    def rng(x):
+        return (x[0], x[1], x[2])
+
+    def bk(*xs):
+        return [b for x in xs if x[0] == "ps" for b in range(x[1] // 512, (x[2] - 1) // 512 + 1)]
+
+    def split(rs):
+        return [rng(x) for x in rs if x[0] != "ps"]
+
+    def tt(out, a, b, o):
+        op("V", lambda e: e.tensor_tensor(ap(out), ap(a), ap(b), o), split((a, b)), split((out,)), bk(out, a, b))
+
+    def ts(out, a, s1, s2, o0, o1=None):
+        c1 = ap(s1) if isinstance(s1, tuple) else s1
+        c2 = ap(s2) if isinstance(s2, tuple) else s2
+        R = split([a] + [s for s in (s1, s2) if isinstance(s, tuple)])
+        if o1 is None:
+            op("V", lambda e: e.tensor_scalar(ap(out), ap(a), c1, None, o0), R, split((out,)), bk(out, a))
+        else:
+            op("V", lambda e: e.tensor_scalar(ap(out), ap(a), c1, c2, o0, o1), R, split((out,)), bk(out, a))
+
+    def vcopy(out, a):
+        op("V", lambda e: e.tensor_copy(ap(out), ap(a)), split((a,)), split((out,)), bk(out, a))
+
+    def act(out, a, func=AF.Copy):
+        op("S", lambda e: e.activation(ap(out), ap(a), func), split((a,)), split((out,)), bk(out, a))
+
+    def vscan(out, a, b, o0, o1):
+        op("V", lambda e: e.tensor_tensor_scan(ap(out), ap(a), ap(b), 0.0, o0, o1), split((a, b)), split((out,)), bk(out, a, b))
+
+    def gather(q, out, wn, off):
+        w, o = T[wn[0]][:, wn[1]:wn[2]], T[off[0]][:, off[1]:off[2]]
+        if q == "V":
+            op("V", lambda e: e.tensor_copy(ap(out), w.indirect(o)), [wn, off], [rng(out)])
+        else:
+            op("S", lambda e: e.activation(ap(out), w.indirect(o), AF.Copy), [wn, off], [rng(out)])
+
+    def mm(out, lhs, rhs, start, stop):
+        return (ap(out), ap(lhs), ap(rhs), start, stop, [rng(lhs), rng(rhs)])
+
+    def iota(n, lo, hi, pattern, base, cm):
+        w = {} if n in INTS else {"allow_small_or_imprecise_dtypes": True}
+        op("G", lambda e: e.iota(T[n][:, lo:hi], pattern, base, cm, **w), (), [(n, lo, hi)])
+
+    PTS, WR = ("ptx", 16, 4112), ("wr", 16, 272)
+
+    dma("Y", T.w0r[0:8, :], T.w0[:, :], (), [full("w0r")])
+    dma("S", T.ptx[:, 16:4112], T.pt[:], (), [PTS])
+    for h, n in enumerate(("zs", "zh")):
+        dma("Y", T[n][:], T.lm[:, h * 512:h * 512 + 512], (), [full(n)])
+    dma("Y", T.zo[:], T.z0[:], (), [full("zo")])
+    for a in (("az01", rank + 1, "zin", 0, 512), ("az2", rank + 2, "zin", 512, 768), ("az3", rank + 3, "zin", 768, 1024),
+              ("ar1", rank + 1, "zrr", 0, 256), ("ar2", rank + 1, "zrr", 256, 512), ("af0", rank - 1, "fin", 0, 256),
+              ("af1", rank - 2, "fin", 256, 512), ("af2", rank - 3, "fin", 512, 768), ("af3", rank - 3, "fin", 768, 1024)):
+        arrive(*a)
+
+    iota("dw", 0, 128, [[1, 128]], 0, -16)
+    iota("ip", 0, 128, [[0, 128]], 0, 1)
+    iota("ij", 0, 128, [[1, 128]], 0, 0)
+    iota("j16", 0, 256, [[16, 256]], 0, 0)
+    iota("hx", 0, 512, [[0, 2], [976, 256]], 0, 0)
+    for k in range(4):
+        iota("vals", k * 1024, k * 1024 + 1024, [[1, 64], [0, 16]], 64 * k, 0)
+    send(rank - 1, T.zin[:, 0:512], T.zo[:, 0:512], "az01", [full("zo")])
+    send(rank - 2, T.zin[:, 512:768], T.zo[:, 512:768], "az2", [full("zo")])
+    send(rank - 3, T.zin[:, 768:1024], T.zo[:, 768:1024], "az3", [full("zo")])
+    iota("kmx", 0, 2048, [[0, 128], [256, 16]], 0, 0)
+    iota("kmn", 0, 2048, [[0, 128], [-256, 16]], 256, 0)
+
+    for b in range(16):
+        op("V", lambda e: e.tensor_scalar(T.ind[0:8, b * 128:b * 128 + 128], T.dw[0:8, :], float(b), None, OP.is_equal),
+           [full("dw")], [sq("ind", b)])
+    ip, ij, pg, pb, jg, jb = [sq(n) for n in ("ip", "ij", "pg", "pb", "jg", "jb")]
+    tt(sq("idm"), ip, ij, OP.is_equal)
+    ts(pg, ip, 4, None, OP.arith_shift_right)
+    ts(jg, ij, 4, None, OP.arith_shift_right)
+    ts(pb, ip, 15, None, OP.bitwise_and)
+    tt(sq("lt"), ip, ij, OP.is_lt)
+    ts(sq("nid"), sq("idm"), -1.0, None, OP.mult)
+    tt(sq("bo"), pg, jg, OP.is_equal)
+    ts(jb, ij, 15, None, OP.bitwise_and)
+    vcopy(("pbc", 0, 1), ("pb", 0, 1))
+    tt(sq("tri"), sq("lt"), sq("bo"), OP.mult)
+    tt(("colb", 0, 16), ("pb", 0, 16), ("ij", 0, 16), OP.is_equal)
+    ts(full("lim"), full("j16"), ("pbc", 0, 1), 8192.0, OP.add, OP.add)
+    tt(sq("tru"), sq("bo"), sq("tri"), OP.subtract)
+    for n in ("ptx", "wr"):
+        op("V", lambda e: e.memset(T[n][:, 0:16], 0.0), (), [(n, 0, 16)])
+    op("V", lambda e: e.memset(T.win[:, 0:8192], 0.0), (), [("win", 0, 8192)])
+
+    group(7, [(ps[:, 3584:3840], T.ind[0:8, b * 128:b * 128 + 128], T.w0r[0:8, b::16], b == 0, b == 15, [sq("ind", b), full("w0r")])
+              for b in range(16)])
+    act(WR, ("ps", 3584, 3840))
+
+    def starts():
+        group(7, [mm(("ps", 3584, 3840), sq("tri"), WR, True, False),
+                  mm(("ps", 3584, 3840), sq("tru"), ("wr", 15, 271), False, True)])
+        group(7, [mm(("ps", 3840, 4096), sq("bo"), WR, True, True)])
+        vscan(full("st"), ("ps", 3584, 3840), full("lim"), OP.add, OP.min)
+        vcopy(full("stu"), full("st"))
+
+    def scatter():
+        op("V", lambda e: e.tensor_copy(T.win[:, 0:12288].indirect(T.stu[:, 0:256]), T.dif[:]),
+           [full("stu"), full("dif")], [full("win")])
+
+    def totals_t():
+        op("V", lambda e: e.tensor_reduce(T.sm[:, 0:1], ps[:, 3840:4096], AxisListType.X, OP.add), (), [("sm", 0, 1)], [7])
+        ts(("sm", 1, 2), ("sm", 0, 1), 8192.0, 0.5, OP.min, OP.mult)
+        ts(("si", 0, 1), ("sm", 1, 2), -0.25, None, OP.add)
+        ts(("t2", 0, 1), ("si", 0, 1), 1.0 / 2048, None, OP.mult)
+
+    def expand_seq():
+        vscan(full("ex"), ("win", 0, 8192), ("win", 0, 8192), OP.add, OP.max)
+
+    def expand_w():
+        for h in range(4):
+            o = (h % 3) * 1024
+            for b in range(4 * h, 4 * h + 4):
+                c = o + (b % 4) * 256
+                group(c // 512, [mm(("ps", c, c + 256), sq("xpd", b), WR, True, True)])
+            for b in range(4 * h, 4 * h + 4):
+                c = o + (b % 4) * 256
+                op("S", lambda e: e.activation(T.nat[:, b::16], ps[:, c:c + 256], AF.Copy), (), [("nat", b, b + 1)], [c // 512])
+
+    def hash_products(zr):
+        for kk in range(2):
+            o = 3584 + kk * 256
+            group(7, [mm(("ps", o, o + 256), sq("uhi"), zr, True, False), mm(("ps", o, o + 256), sq("ulo"), zr, False, kk == 0)]
+                  + ([mm(("ps", o, o + 256), sq("u128"), zr, False, True)] if kk else []))
+
+    mbuf = ("w0r", "ptx")
+
+    def members(place, t):
+        for m in MEMBERS.get((place, t), []):
+            gather("S", (mbuf[m], 0, 4096), full("nat"), half("lmu", t + m))
+
+    def member_sum(m, bank):
+        o = bank * 512 + 256 * m
+        group(bank, [mm(("ps", o, o + 256), sq("idm"), (mbuf[m], b, 4096, 16), b == 0, b == 15) for b in range(16)])
+
+    def member_light(m, bank):
+        o = bank * 512 + 256 * m
+        ts(half("lfl", m), ("ps", o, o + 256), 23.5, None, OP.is_lt)
+
+    wraps = []
+
+    def pieces(place, t):
+        for c, k in PIECES.get((place, t), []):
+            op("S", lambda e: e.activation(T.invw[:, 0:4096].indirect(T.lmu[:, c * 256 + 64 * k:c * 256 + 64 * k + 64]),
+                                           T.vals[:, k * 1024:(k + 1) * 1024], AF.Silu),
+               [full("lmu"), half("vals", k, 1024)], [full("invw")])
+            if k == 3:
+                dma("G", T.rbf[:], T.invw[:], [full("invw")], [full("rbf")])
+                wraps.append(c)
+
+    def inv_wrap(bank):
+        while wraps:
+            c = wraps.pop()
+            o = bank * 512
+            group(bank, [mm(("ps", o, o + 256), sq("edg", b), ("rbf", b, 4096, 16), b == 0, b == 15) for b in range(16)])
+            vcopy(full("ivi"), ("ps", o, o + 256))
+            vcopy(half("inv", c), full("ivi"))
+
+    for h, n in enumerate(("zs", "zh")):
+        vcopy(half("lmu", h, 512), full(n))
+    starts()
+    for c in range(8 - DV):
+        o = (c % 6) * 512
+        group(c % 6, [mm(("ps", o, o + 512), sq("idm"), ("ptx", c * 512 + 16, c * 512 + 528), True, False),
+                      mm(("ps", o, o + 512), sq("nid"), ("ptx", c * 512 + 15, c * 512 + 527), False, True)])
+        act(half("dif", c, 512), ("ps", o, o + 512))
+    tt(("dif", 4096 - 512 * DV, 4096), ("ptx", 4112 - 512 * DV, 4112), ("ptx", 4111 - 512 * DV, 4111), OP.subtract)
+    scatter()
+    pieces("setup", 0)
+    for b in range(16):
+        op("S", lambda e: e.activation(T.xpd[:, b * 128:b * 128 + 128], T.bo[:], AF.Copy, scale=T.colb[:, b:b + 1]),
+           [full("bo"), full("colb")], [sq("xpd", b)])
+    totals_t()
+    ci1, ci2, ci3, ci4 = [sq(n) for n in ("ci1", "ci2", "ci3", "ci4")]
+    ts(ci1, pb, 2.0, 1.0, OP.mult, OP.add)
+    ts(ci2, jb, 8.0, 7.0, OP.mult, OP.add)
+    ts(full("hx"), full("hx"), 65535, None, OP.bitwise_and)
+    tt(ci3, ci1, ci2, OP.mult)
+    ts(sq("aid"), sq("idm"), ALPHA, None, OP.mult)
+    ts(ci4, ci3, 65504, None, OP.bitwise_and)
+    ts(ci2, ci1, 128.0, None, OP.mult)
+    tt(sq("uhi"), ci4, sq("bo"), OP.mult)
+    ts(ci4, ci3, 31, None, OP.bitwise_and)
+    ts(sq("nad"), sq("idm"), -ALPHA, None, OP.mult)
+    tt(sq("ulo"), ci4, sq("bo"), OP.mult)
+    tt(sq("u128"), ci2, sq("bo"), OP.mult)
+    vcopy(full("cf"), full("hx"))
+    hash_products(("zin", 0, 256))
+    expand_seq()
+    iota("win", 0, 8192, [[0, 8192]], 0, 0)
+    expand_w()
+
+    for t in range(3):
+        last = t == 2
+        zr = [("zin", 0, 256), ("zrr", 0, 256), ("zrr", 256, 512)][t]
+        zt = half("zin", t + 1)
+        pre = MEMBERS[("pre", t)]
+        late = [m for m in range(2) if m not in pre]
+        members("pre", t)
+        for n, z in (("zx0", zr), ("zx1", zt)):
+            for j in range(2):
+                op("S", lambda e: e.activation(T[n][:, j::2], ap(z), AF.Copy), [rng(z)], [(n, j, j + 1)])
+        for k in range(2):
+            tt(half("hx", k), ("ps", 3584 + 256 * k, 3840 + 256 * k), half("cf" if t == 0 else "ca", k), OP.add)
+        for k in range(2):
+            ts(half("hy", k), half("hx", k), 4, 4095, OP.arith_shift_right, OP.bitwise_and)
+        for k in range(2):
+            ts(half("hx", k), half("hy", k), ("t2", 0, 1), -4095.5 + 1.0 / 4096, OP.mult, OP.add)
+        for k in range(2):
+            ts(half("hu", k), half("hx", k), 4095.0, None, OP.add)
+        pieces("net", t)
+        for k in range(4):
+            gather(NETQ[t][k], half("net", k, 2048), full("ex"), half("hu", k, 128))
+        for m in pre:
+            member_sum(m, 6)
+        if t == 0:
+            tt(("b8", 0, 8), ("pg", 0, 8), ("ij", 0, 8), OP.is_equal)
+            ts(ci3, ip, 7, None, OP.bitwise_and)
+
+        nab, inds = [0], {}
+
+        def differences(v):
+            e = (v // 8) * 4096 + 4096
+            for h in range(2):
+                o = (v % 3) * 1024 + h * 512
+                b0 = e - 4096 + (v // 2 % 4) * 2 + h
+                group(o // 512, [mm(("ps", o, o + 512), sq("nad"), full("zx%d" % (v % 2)), True, False),
+                                 mm(("ps", o, o + 512), sq("aid"), ("net", b0, e, 8), False, True)])
+
+        def near(v):
+            i = half("ind", v % 6, 1024)
+            p = half("ps", v % 3, 1024)
+            if v in VUNITS[t]:
+                ts(i, p, 12582912.0, 12582912.0, OP.add, OP.is_equal)
+                return
+            a = half("ab", nab[0] % 4, 1024)
+            nab[0] += 1
+            act(a, p, AF.Abs)
+            ts(i, a, 0.5, None, OP.is_le)
+
+        def counts(v):
+            r = v % 2
+            for h in range(2):
+                for lb in range(2):
+                    for j in range(2):
+                        c = (6 + r) * 512 + lb * 256 + ((v // 8) * 16 + (v // 2 % 4) * 2 + h + 8 * j) * 8
+                        i = (v % 6) * 1024 + h * 512 + lb * 256
+                        group(6 + r, [mm(("ps", c, c + 8), ("ind", i + j, i + 256, 2), ("b8", 0, 8), True, True)])
+
+        def scans(kk, which):
+            k, n, o0, o1 = ("kmx", "tmx", OP.min, OP.max) if which == 0 else ("kmn", "tmn", OP.max, OP.min)
+            for h in range(2):
+                vscan(half(n, h, 2048), full(k), half("net", 2 * kk + h, 2048), o0, o1)
+            if kk == 0:
+                vcopy(full("mn0" if which else "mx0"), (n, 15, 4096, 16))
+            elif which == 0:
+                tt(full("mxx"), full("mx0"), (n, 15, 4096, 16), OP.max)
+            else:
+                tt(full("mnn"), full("mn0"), (n, 15, 4096, 16), OP.min)
+
+        for s in range(16 + LAG):
+            if s < 16:
+                differences(s)
+                near(s)
+            members(s, t)
+            pieces(s, t)
+            if s == 1:
+                for m in pre:
+                    member_light(m, 6)
+            if s in WRAP[t]:
+                inv_wrap(6 if s < 2 else 3)
+            if s == LATE:
+                for m in late:
+                    member_sum(m, 2)
+            if s >= LAG:
+                counts(s - LAG)
+            if s == 0 and t == 0:
+                tt(sq("b2"), ci3, jg, OP.is_equal)
+                for b in range(16):
+                    ts(sq("edg", b), sq("idm"), ("colb", b, b + 1), None, OP.mult)
+            if s in SCANS:
+                scans(*SCANS[s])
+            if s == 12:
+                tt(full("ivi"), full("mxx"), full("mnn"), OP.add)
+                ts(full("yy"), full("ivi"), 1, None, OP.arith_shift_right)
+            if s == 16:
+                for m in late:
+                    member_light(m, 2)
+                for r, z in ((0, zr), (1, zt)):
+                    tt(half("zs", r), z, full("yy"), OP.add)
+                for r in range(2):
+                    ts(half("zh", r), half("zs", r), 1, None, OP.arith_shift_right)
+                for r, z in ((0, zr), (1, zt)):
+                    tt(half("zd", r), half("zh", r), z, OP.subtract)
+        for r in range(2):
+            ts(half("h01", r, 512), ("ps", (6 + r) * 512, (7 + r) * 512), 11.5, None, OP.is_ge)
+        for r in range(2):
+            for lb in range(2):
+                c = 2048 + r * 256 + lb * 128
+                group(4, [mm(("ps", c, c + 128), sq("h01", r * 4 + lb * 2 + k), sq("idm"), k == 0, k == 1) for k in range(2)])
+        vcopy(full("hts"), ("ps", 2048, 2560))
+        group(5, [mm(("ps", 2560, 3072), sq("b2"), full("hts"), True, True)])
+        s0, s1, l0, l1 = half("sel", 0), half("sel", 1), half("lg", 0), half("lg", 1)
+        ts(s0, ("ps", 2560, 2816), 0.5, None, OP.is_lt)
+        ts(full("m1"), ("ps", 2816, 3072), 0.5, None, OP.is_lt)
+        tt(l0, s0, half("lfl", 0), OP.mult)
+        tt(s1, full("m1"), s0, OP.is_gt)
+        tt(l1, s1, half("lfl", 1), OP.mult)
+        for k in range(4):
+            gather("S", half("w0r", k, 1024), l0, half("inv", t * 4 + k, 64))
+            gather("V", half("ptx", k, 1024), l1, half("inv", t * 4 + 4 + k, 64))
+        for k in range(4):
+            c = 3072 + 64 * k
+            group(6, [mm(("ps", c, c + 64), sq("edg", b), (mbuf[m], k * 1024 + b, k * 1024 + 1024, 16), b == 0 and m == 0, b == 15 and m == 1)
+                      for m in range(2) for b in range(16)])
+        for k, (x, f) in enumerate(((s0, 1.0), (s1, 1.0), (l0, -1.0), (l1, -1.0))):
+            op("S", lambda e: e.activation(T.h01[:, k * 256:k * 256 + 256], ap(x), AF.Identity, scale=f, accum_out=T.acc[:, k:k + 1]),
+               [x], [half("h01", k), ("acc", k, k + 1)])
+        pieces("marks", t)
+        for r in range(2):
+            tt(half("zm", r), half("sel", r), half("zd", r), OP.mult)
+        for r, z in ((0, zr), (1, zt)):
+            o = half("znew", 2 * t + r)
+            tt(o, half("zm", r), z, OP.add)
+            if r == 0:
+                send(rank + 1 + t, ap(half("fin", t)), ap(o), "af%d" % t, [o])
+            elif not last:
+                send(rank - 1, ap(half("zrr", t)), ap(o), "ar%d" % (t + 1), [o])
+            else:
+                send(rank - 1, ap(half("fin", 3)), ap(o), "af3", [o])
+        ts(full("wf"), ("ps", 3072, 3328), 0.5, 1.0, OP.is_ge, OP.add)
+        tt(full("wt"), WR, full("wf"), OP.mult)
+        ts(full("w1"), full("wt"), 8.0, None, OP.min)
+        group(3, [mm(("ps", 1536, 1792), sq("bo"), full("w1"), True, True)])
+        op("V", lambda e: e.tensor_reduce(T.sm[:, 2:3], ps[:, 1536:1792], AxisListType.X, OP.add), (), [("sm", 2, 3)], [3])
+        ts(("hv", 0, 1), ("sm", 2, 3), 7168.5, -0.5, OP.is_gt, OP.mult)
+        ts(("sc", 0, 1), ("hv", 0, 1), 1.0, None, OP.add)
+        ts(("bi", 0, 1), ("hv", 0, 1), -0.5, 128.0, OP.mult, OP.add)
+        ts(full("w2"), full("w1"), ("sc", 0, 1), ("bi", 0, 1), OP.mult, OP.add)
+        ts(WR, full("w2"), -128.0, None, OP.add)
+        if not last:
+            starts()
+            scatter()
+            totals_t()
+            expand_w()
+            hash_products(half("zrr", t))
+        op("V", lambda e: e.tensor_reduce(T.yat[:, t:t + 1], T.acc[:, 0:4], AxisListType.X, OP.add), [("acc", 0, 4)], [("yat", t, t + 1)])
+        if not last:
+            ts(("a16", 0, 1), ("yat", t, t + 1), 16.0, None, OP.mult)
+            ts(full("ca"), full("cf"), ("a16", 0, 1), None, OP.add)
+            expand_seq()
+            if t == 0:
+                iota("win", 0, 8192, [[0, 8192]], 0, 0)
+
+    dma("Y", T.ya[:, :], T.yat[0:128:16, 0:3], [("yat", 0, 3)])
+    for h in range(4):
+        o = (h % 3) * 1024
+        for b in range(4 * h, 4 * h + 4):
+            c = o + (b % 4) * 256
+            group(c // 512, [(ps[0:8, c:c + 256], T.xpd[:, b * 128:b * 128 + 128:16], T.wr[:, 16:272], True, True, [sq("xpd", b), WR])])
+        for b in range(4 * h, 4 * h + 4):
+            c = o + (b % 4) * 256
+            if b % 4 < 2:
+                op("S", lambda e: e.activation(T.vals[0:8, b::16], ps[0:8, c:c + 256], AF.Copy), (), [("vals", b, b + 1)], [c // 512])
+            else:
+                op("V", lambda e: e.tensor_copy(T.vals[0:8, b::16], ps[0:8, c:c + 256]), (), [("vals", b, b + 1)], [c // 512])
+    dma("Y", T.yw[:, :], T.vals[0:8, :], [full("vals")])
+    for c in range(4):
+        dma("Y", ap(("yz", c * 256, c * 256 + 256)), ap(half("fin", c)), [half("fin", c)])
+    for s, v in totals.items():
+        if known["G"].get(s, 0) < v:
+            g.wait_ge(T.sem[s], v)
+            known["G"][s] = v

@@ -1,32 +1,36 @@
+from concourse.bass import DstId, RemoteDMATransfer
 from concourse.mybir import AluOpType, AxisListType, ActivationFunctionType
 
 OP = AluOpType
 AF = ActivationFunctionType
 ALPHA = 226.0 / 32768.0
+MAGIC = 12582912.0
+BASE = 65536.0 + 255.5
 
-PIECES = {("setup", 0): [(0, 0), (0, 1), (0, 2), (0, 3)], (2, 0): [(1, 0)], (4, 0): [(1, 1)], (5, 0): [(1, 2)], (6, 0): [(1, 3)],
-          ("marks", 0): [(2, 0), (2, 1), (2, 2)], (3, 1): [(2, 3)],
-          ("marks", 1): [(3, 0), (3, 1), (3, 2)], (3, 2): [(3, 3)]}
-WRAP = {0: [1, 15], 1: [15], 2: [15]}
-LATE = 14
-VUNITS = {0: [0, 2, 3, 4, 6, 7, 8, 10, 11, 12, 14, 15], 1: [4, 8, 12], 2: [4, 8, 12]}
-NETQ = ["VVVV", "VSVS", "VSVS"]
-MEMBERS = {("pre", 0): [0], (9, 0): [1], ("pre", 1): [0, 1], ("pre", 2): [0, 1]}
-SCANS = {2: (0, 0), 4: (0, 1), 8: (1, 0), 10: (1, 1)}
-DV = 2
-LAG = 3
+TASKS = {("setup", 0): [("inv", "S", c, k) for c in range(2) for k in range(4)],
+         ("net", 0): [("mem", "S", 0), ("mem", "S", 1)], ("net", 1): [("mem", "S", 0), ("mem", "S", 1)], ("net", 2): [("mem", "S", 0), ("mem", "S", 1)],
+         ("tail", 0): [("inv", "S", 2, 0), ("inv", "S", 2, 1)], ("post", 0): [("inv", "S", 2, 2), ("inv", "S", 2, 3)],
+         ("tail", 1): [("inv", "S", 3, 0), ("inv", "S", 3, 1)], ("post", 1): [("inv", "S", 3, 2), ("inv", "S", 3, 3)]}
+FQ = ["VVVV", "SSSV", "SSSV"]
+NETQ = ["VVVVSSSS", "SVSSSSSS", "SVSSSSSS"]
+NETV = [[0, 0, 1, 3], [0], [0]]
+SUMS = {0: {0: 13, 1: 16}, 1: {0: 13, 1: 16}, 2: {0: 13, 1: 16}}
+LAG = 2
+NSEND = 8
+NFOLD = 8
 
 
 def _table():
     out = {"ps": ("psum", [128, 4096], "float32")}
-    for d, cols in (("bfloat16", "w0r:4096 ptx:4112 dif:4096 win:12288 ex:8192 net:8192 tmx:4096 tmn:4096 kmx:2048 kmn:2048 ab:4096 ind:6144"
-                     " nat:4096 rbf:4096 zo:1024 zin:1024 zrr:512 fin:1024 znew:1536 edg:2048 xpd:2048 idm:128 nid:128 aid:128 nad:128 bo:128"
-                     " lt:128 tri:128 tru:128 b8:16 b2:128 uhi:128 ulo:128 u128:128 wr:272 wf:256 wt:256 w1:256 w2:256 zx0:512 zx1:512"
-                     " h01:1024 hts:512 sel:512 m1:256 lg:512 lfl:512 mx0:256 mn0:256 mxx:256 mnn:256 zd:512 zm:512"),
-                    ("float32", "invw:4096 vals:4096 colb:16 pbc:16 cf:512 ca:512 lim:256 st:256 sm:16 t2:16 hv:16 sc:16 bi:16 acc:16 yat:16 a16:16"),
-                    ("int32", "ip:128 ij:128 pg:128 pb:128 jg:128 jb:128 dw:128 ci1:128 ci2:128 ci3:128 ci4:128 j16:256 si:16 hx:512 hy:512"
-                     " yy:256 zs:512 zh:512 ivi:256"),
-                    ("uint16", "lmu:1024 inv:1024 stu:256 hu:512")):
+    for d, cols in (("bfloat16", "ptx:4096 win:4352 dfl:1088 scn:4096 ff:4096 net:8192 ind:6144 nat:4096 mg0:4096 mg1:4096 oh0:4096 oh1:4096"
+                     " oh2:4096 zo:1024 zin:1024 zrr:512 fin:1024 znew:1536 hb:1536 mm:1536 m16:2048 idm:128 nid:128 hid:128 eid:128"
+                     " aid:128 nad:128 bo:128 lt:128 tri:128 key:128 one:128 mon:128 e16:128 cm:256 x8:128 xs:144 xu:144 xy:144 b16:16 s8:16"
+                     " kap:32 kmx:512 nh:256 dd:256 wr:256 w1:256 w2:256 w2x:256 jj:256 jf:256 cmx:1024 selh:32 lth:32 fh:32 nsl:16"
+                     " inn:16 wd:32 bt:1024 st8:512 yy:256 yz2:512 ee:512 wt:256 tw:16 eps:512 sid:128 dz:256"),
+                    ("float32", "inv0:4096 inv1:4096 vals:4096 pre:272 y0:272 ltf:272 cc:288 qq:512 lim:16 col:16 sm:16 tau:16 rr:16 sc:16"
+                     " a8:16 ar:16 yat:16 cw0:16 cw:16 p2:16 p8:16 cf:16 wo:256 j143:144"),
+                    ("int32", "ip:128 ij:128 pg:128 pb:128 jg:128 jb:128 dw:144 d8:16 j16:16 jd:256 si:16 ci:16 cj:16 hx:512 hy:512 lmi:1024"),
+                    ("uint16", "lmu:1024 stu:16 fu:256 hu:512")):
         for c in cols.split():
             n, w = c.split(":")
             out[n] = ("sbuf", [128, int(w)], d)
@@ -35,15 +39,38 @@ def _table():
 
 SCRATCH = _table()
 INTS = [n for n in SCRATCH if SCRATCH[n][2] == "int32"]
-NDMA = 16
+NDMA = 40
 SEMAPHORES = (["qv", "qs", "qp", "qg", "sent", "az01", "az2", "az3", "ar1", "ar2", "af0", "af1", "af2", "af3"]
-              + ["d%d" % k for k in range(NDMA)])
+              + ["%s%d" % (n, t) for n in ("fo", "hf", "am") for t in range(3)] + ["d%d" % k for k in range(NDMA)])
 QSEM = {"V": "qv", "S": "qs", "P": "qp", "G": "qg"}
+
+
+def helpers(cores, topo):
+    out = []
+    for c in cores:
+        out.append([h for h in topo.cores_of(c) if topo.die(h) == topo.die(c) and h not in cores and h not in out][0])
+    return out
+
+
+def bits(engines):
+    m = 0
+    for e in engines:
+        m |= 1 << e
+    return m
 
 
 def rank_program(g, core, T, topo):
     rank = T.rank_of(core)
+    hands = helpers(list(T.cores), topo)
     if rank is None:
+        if core in hands:
+            dst = T.cores[hands.index(core)]
+            rid, pid = topo.addr(dst)[:2]
+            for t in range(3):
+                g.wait_ge(T.sem["hf%d" % t], 2 * NFOLD)
+                g.remote_dma(T.mm[:, 512 * t:512 * t + 512], T.hb[:, 512 * t:512 * t + 512], T.sem["am%d" % t], T.sem.sent, pid, rid,
+                             bits(topo.engines(core, dst)[:NSEND]))
+            g.wait_ge(T.sem.sent, 3 * NSEND)
         return
     eng = {"V": g.vector, "S": g.scalar, "P": g.tensor, "G": g, "Y": g.sync}
     known = {q: {} for q in eng}
@@ -101,27 +128,38 @@ def rank_program(g, core, T, topo):
         for o, l, r, a, b, R in mats:
             note("P", tok, R, (), (bank,))
 
-    def dma(q, out, in_, R=(), W=()):
+    def dmas(q, pairs, R=(), W=()):
         wait(q, deps(q, R, W, ()))
         s = "d%d" % ndma[0]
         ndma[0] += 1
-        eng[q].dma_start(out, in_).then_inc(T.sem[s], 16)
-        note(q, token(q, s, 16), R, W, ())
+        for out, in_ in pairs:
+            eng[q].dma_start(out, in_).then_inc(T.sem[s], 16)
+        note(q + s, token(q, s, 16 * len(pairs)), R, W, ())
+
+    def dma(q, out, in_, R=(), W=()):
+        dmas(q, [(out, in_)], R, W)
 
     def send(to, out, in_, sem, R):
         dst = T.cores[to % len(T.cores)]
         wait("G", deps("G", R, (), ()))
         rid, pid = topo.addr(dst)[:2]
-        m = 0
-        for e in topo.engines(core, dst)[:8]:
-            m |= 1 << e
-        g.remote_dma(out, in_, T.sem[sem], T.sem.sent, pid, rid, m)
-        totals["sent"] = totals.get("sent", 0) + bin(m).count("1")
+        g.remote_dma(out, in_, T.sem[sem], T.sem.sent, pid, rid, bits(topo.engines(core, dst)[:NSEND]))
+        totals["sent"] = totals.get("sent", 0) + NSEND
 
-    def arrive(sem, frm, name, lo, hi):
-        n = len(topo.engines(T.cores[frm % len(T.cores)], core)[:8])
-        totals[sem] = n
-        recs.setdefault(name, []).append((lo, hi, "w", (sem, n, {sem: n}), "net"))
+    def fold(t):
+        dst = hands[rank]
+        wait("G", deps("G", [full("net")], (), ()))
+        rid, pid = topo.addr(dst)[:2]
+        en = topo.engines(core, dst)
+        g.remote_dma_fused([RemoteDMATransfer(dst_ids=[DstId(rid=rid, pnc=pid)], dma_engine_mask=bits(en[h * NFOLD:h * NFOLD + NFOLD]),
+                                              remote_sem=T.sem["hf%d" % t], srcs=[T.net[:, k * 256:k * 256 + 256] for k in range(32)],
+                                              dsts=[T.hb[:, 512 * t + 256 * h:512 * t + 256 * h + 256]], alu_op=2 + h) for h in range(2)],
+                           local_sem=T.sem["fo%d" % t])
+        note("fold", token("G", "fo%d" % t, 2 * NFOLD), [full("net")], (), ())
+
+    def arrive(sem, name, lo, hi):
+        totals[sem] = NSEND
+        recs.setdefault(name, []).append((lo, hi, "w", (sem, NSEND, {sem: NSEND}), "net"))
 
     def full(n):
         return (n, 0, SCRATCH[n][1][1])
@@ -132,9 +170,15 @@ def rank_program(g, core, T, topo):
     def sq(n, b=0):
         return (n, b * 128, b * 128 + 128)
 
-    def ap(x):
+    def col(n, c=0):
+        return (n, c, c + 1)
+
+    def pr(lo, w, step=None):
+        return ("ps", lo, lo + w) if step is None else ("ps", lo, lo + w, step)
+
+    def ap(x, parts=128):
         n, lo, hi = x[0], x[1], x[2]
-        return T[n][:, lo:hi:x[3]] if len(x) > 3 else T[n][:, lo:hi]
+        return T[n][0:parts, lo:hi:x[3]] if len(x) > 3 else T[n][0:parts, lo:hi]
 
     def rng(x):
         return (x[0], x[1], x[2])
@@ -143,373 +187,367 @@ def rank_program(g, core, T, topo):
         return [b for x in xs if x[0] == "ps" for b in range(x[1] // 512, (x[2] - 1) // 512 + 1)]
 
     def split(rs):
-        return [rng(x) for x in rs if x[0] != "ps"]
+        return [rng(x) for x in rs]
 
     def tt(out, a, b, o):
         op("V", lambda e: e.tensor_tensor(ap(out), ap(a), ap(b), o), split((a, b)), split((out,)), bk(out, a, b))
 
-    def ts(out, a, s1, s2, o0, o1=None):
-        c1 = ap(s1) if isinstance(s1, tuple) else s1
-        c2 = ap(s2) if isinstance(s2, tuple) else s2
-        R = split([a] + [s for s in (s1, s2) if isinstance(s, tuple)])
-        if o1 is None:
-            op("V", lambda e: e.tensor_scalar(ap(out), ap(a), c1, None, o0), R, split((out,)), bk(out, a))
-        else:
-            op("V", lambda e: e.tensor_scalar(ap(out), ap(a), c1, c2, o0, o1), R, split((out,)), bk(out, a))
+    def ts(out, a, s1, s2, o0, o1=None, W=None, parts=128):
+        c1 = ap(s1, parts) if isinstance(s1, tuple) else s1
+        c2 = ap(s2, parts) if isinstance(s2, tuple) else s2
+        R = [a] + [s for s in (s1, s2) if isinstance(s, tuple)]
+        args = (c1, None, o0) if o1 is None else (c1, c2, o0, o1)
+        op("V", lambda e: e.tensor_scalar(ap(out, parts), ap(a, parts), *args), split(R), W or split((out,)), bk(out, *R))
 
     def vcopy(out, a):
         op("V", lambda e: e.tensor_copy(ap(out), ap(a)), split((a,)), split((out,)), bk(out, a))
 
-    def act(out, a, func=AF.Copy):
-        op("S", lambda e: e.activation(ap(out), ap(a), func), split((a,)), split((out,)), bk(out, a))
+    def vset(out, c):
+        op("V", lambda e: e.memset(ap(out), c), (), split((out,)))
 
-    def vscan(out, a, b, o0, o1):
-        op("V", lambda e: e.tensor_tensor_scan(ap(out), ap(a), ap(b), 0.0, o0, o1), split((a, b)), split((out,)), bk(out, a, b))
+    def act(out, a, func=AF.Copy, parts=128, **kw):
+        op("S", lambda e: e.activation(ap(out, parts), ap(a, parts), func, **kw), split((a,)), split((out,)), bk(out, a))
+
+    def vscan(out, a, b, init, o0, o1):
+        R = [a, b] + ([init] if isinstance(init, tuple) else [])
+        op("V", lambda e: e.tensor_tensor_scan(ap(out), ap(a), ap(b), ap(init) if isinstance(init, tuple) else init, o0, o1),
+           split(R), split((out,)), bk(out, a, b))
+
+    def vsum(out, a):
+        op("V", lambda e: e.tensor_reduce(ap(out), ap(a), AxisListType.X, OP.add), split((a,)), split((out,)), bk(out, a))
 
     def gather(q, out, wn, off):
-        w, o = T[wn[0]][:, wn[1]:wn[2]], T[off[0]][:, off[1]:off[2]]
+        w, o = ap(wn), ap(off)
         if q == "V":
             op("V", lambda e: e.tensor_copy(ap(out), w.indirect(o)), [wn, off], [rng(out)])
         else:
             op("S", lambda e: e.activation(ap(out), w.indirect(o), AF.Copy), [wn, off], [rng(out)])
 
-    def mm(out, lhs, rhs, start, stop):
-        return (ap(out), ap(lhs), ap(rhs), start, stop, [rng(lhs), rng(rhs)])
+    def mm(out, lhs, rhs, start=True, stop=True, k=128, m=128):
+        return (ap(out, m), ap(lhs, k), ap(rhs, k), start, stop, [rng(lhs), rng(rhs)])
 
-    def iota(n, lo, hi, pattern, base, cm):
+    def iota(n, pattern, base, cm):
         w = {} if n in INTS else {"allow_small_or_imprecise_dtypes": True}
-        op("G", lambda e: e.iota(T[n][:, lo:hi], pattern, base, cm, **w), (), [(n, lo, hi)])
+        op("G", lambda e: e.iota(T[n][:], pattern, base, cm, **w), (), [full(n)])
 
-    PTS, WR = ("ptx", 16, 4112), ("wr", 16, 272)
+    def shifted(n, b):
+        return (n, 15 - b, 143 - b)
 
-    dma("Y", T.w0r[0:8, :], T.w0[:, :], (), [full("w0r")])
-    dma("S", T.ptx[:, 16:4112], T.pt[:], (), [PTS])
-    for h, n in enumerate(("zs", "zh")):
-        dma("Y", T[n][:], T.lm[:, h * 512:h * 512 + 512], (), [full(n)])
+    WR, IDM, NH, B8 = full("wr"), full("idm"), full("nh"), ("b16", 0, 8)
+    PB, C15, ISZ, NZ, JK, DEF, YW, INI, COF = [col("col", k) for k in range(9)]
+
+    dma("Y", T.mg0[0:8, :], T.w0[:, :], (), [full("mg0")])
     dma("Y", T.zo[:], T.z0[:], (), [full("zo")])
-    for a in (("az01", rank + 1, "zin", 0, 512), ("az2", rank + 2, "zin", 512, 768), ("az3", rank + 3, "zin", 768, 1024),
-              ("ar1", rank + 1, "zrr", 0, 256), ("ar2", rank + 1, "zrr", 256, 512), ("af0", rank - 1, "fin", 0, 256),
-              ("af1", rank - 2, "fin", 256, 512), ("af2", rank - 3, "fin", 512, 768), ("af3", rank - 3, "fin", 768, 1024)):
+    dma("S", T.lmi[:], T.lm[:], (), [full("lmi")])
+    dma("S", T.ptx[:], T.pt[:], (), [full("ptx")])
+    for a in (("az01", "zin", 0, 512), ("az2", "zin", 512, 768), ("az3", "zin", 768, 1024), ("ar1", "zrr", 0, 256), ("ar2", "zrr", 256, 512),
+              ("af0", "fin", 0, 256), ("af1", "fin", 256, 512), ("af2", "fin", 512, 768), ("af3", "fin", 768, 1024),
+              ("am0", "mm", 0, 512), ("am1", "mm", 512, 1024), ("am2", "mm", 1024, 1536)):
         arrive(*a)
 
-    iota("dw", 0, 128, [[1, 128]], 0, -16)
-    iota("ip", 0, 128, [[0, 128]], 0, 1)
-    iota("ij", 0, 128, [[1, 128]], 0, 0)
-    iota("j16", 0, 256, [[16, 256]], 0, 0)
-    iota("hx", 0, 512, [[0, 2], [976, 256]], 0, 0)
-    for k in range(4):
-        iota("vals", k * 1024, k * 1024 + 1024, [[1, 64], [0, 16]], 64 * k, 0)
+    iota("ip", [[0, 128]], 0, 1)
+    iota("jd", [[1, 16], [0, 16]], 0, 0)
+    iota("dw", [[1, 144]], -15, -16)
+    iota("ij", [[1, 128]], 0, 0)
+    iota("j16", [[16, 16]], 0, 0)
+    iota("j143", [[1, 144]], 0, 0)
     send(rank - 1, T.zin[:, 0:512], T.zo[:, 0:512], "az01", [full("zo")])
+    iota("kap", [[8, 32]], 7, 0)
+    iota("d8", [[-16, 16]], 0, 1)
+    iota("nat", [[0, 4096]], 0, 0)
     send(rank - 2, T.zin[:, 512:768], T.zo[:, 512:768], "az2", [full("zo")])
     send(rank - 3, T.zin[:, 768:1024], T.zo[:, 768:1024], "az3", [full("zo")])
-    iota("kmx", 0, 2048, [[0, 128], [256, 16]], 0, 0)
-    iota("kmn", 0, 2048, [[0, 128], [-256, 16]], 256, 0)
+    iota("kmx", [[0, 16], [16, 32]], 0, 0)
 
-    for b in range(16):
-        op("V", lambda e: e.tensor_scalar(T.ind[0:8, b * 128:b * 128 + 128], T.dw[0:8, :], float(b), None, OP.is_equal),
-           [full("dw")], [sq("ind", b)])
     ip, ij, pg, pb, jg, jb = [sq(n) for n in ("ip", "ij", "pg", "pb", "jg", "jb")]
-    tt(sq("idm"), ip, ij, OP.is_equal)
-    ts(pg, ip, 4, None, OP.arith_shift_right)
-    ts(jg, ij, 4, None, OP.arith_shift_right)
+    vset(full("dfl"), 0.0)
+    vset(col("pre"), 0.0)
+    vset(col("cc"), MAGIC)
     ts(pb, ip, 15, None, OP.bitwise_and)
-    tt(sq("lt"), ip, ij, OP.is_lt)
-    ts(sq("nid"), sq("idm"), -1.0, None, OP.mult)
-    tt(sq("bo"), pg, jg, OP.is_equal)
+    ts(pg, ip, 4, None, OP.arith_shift_right)
+    vcopy(PB, col("pb"))
+    ts(full("xs"), full("dw"), 0.0, None, OP.is_equal, parts=8)
+    ts(full("dd"), full("jd"), PB, None, OP.is_equal)
+    ts(ISZ, PB, 0.0, None, OP.is_equal)
+    ts(DEF, ISZ, -1.0, None, OP.add)
+    ts(full("dfl"), full("dfl"), DEF, None, OP.add)
+
+    def clear_window():
+        dmas("Y", [(ap(half("win", k, 1088)), T.dfl[:]) for k in range(4)], [full("dfl")], [full("win")])
+
+    clear_window()
+    dma("Y", T.nat[0:128:16, :], T.w0[:, :], (), [full("nat")])
+    for l in range(16):
+        act(half("vals", l), full("dd"), scale=float(2 ** (20 - l)))
+    group(7, [mm(pr(3584, 256), shifted("xs", b), ("mg0", b, 4096, 16), b == 0, b == 15, k=8) for b in range(16)])
+    ts(jg, ij, 4, None, OP.arith_shift_right)
     ts(jb, ij, 15, None, OP.bitwise_and)
-    vcopy(("pbc", 0, 1), ("pb", 0, 1))
-    tt(sq("tri"), sq("lt"), sq("bo"), OP.mult)
-    tt(("colb", 0, 16), ("pb", 0, 16), ("ij", 0, 16), OP.is_equal)
-    ts(full("lim"), full("j16"), ("pbc", 0, 1), 8192.0, OP.add, OP.add)
-    tt(sq("tru"), sq("bo"), sq("tri"), OP.subtract)
-    for n in ("ptx", "wr"):
-        op("V", lambda e: e.memset(T[n][:, 0:16], 0.0), (), [(n, 0, 16)])
-    op("V", lambda e: e.memset(T.win[:, 0:8192], 0.0), (), [("win", 0, 8192)])
+    ts(NZ, ISZ, -1.0, 1.0, OP.mult, OP.add)
+    tt(full("bo"), pg, jg, OP.is_equal)
+    tt(full("lt"), ip, ij, OP.is_lt)
+    ts(JK, ISZ, 2.0, -1.0, OP.mult, OP.add)
+    tt(full("key"), full("bo"), jb, OP.mult)
+    vcopy(full("lmu"), full("lmi"))
+    tt(full("tri"), full("lt"), full("bo"), OP.mult)
+    for b in range(15):
+        ts(sq("m16", b), full("key"), float(b), None, OP.is_gt)
+        if b == 7:
+            vcopy(WR, pr(3584, 256))
+    ts(full("lim"), full("j16"), PB, MAGIC + 4096.0, OP.add, OP.add)
+    ts(C15, col("pg"), 16.0, 15.0, OP.mult, OP.add)
+    ts(YW, ISZ, 16.0 + 1.0 / 512, -1.0 / 512, OP.mult, OP.add)
+    ts(INI, NZ, BASE + 1.0, None, OP.mult)
+    ts(COF, PB, 2.0, 1.0, OP.mult, OP.add)
 
-    group(7, [(ps[:, 3584:3840], T.ind[0:8, b * 128:b * 128 + 128], T.w0r[0:8, b::16], b == 0, b == 15, [sq("ind", b), full("w0r")])
-              for b in range(16)])
-    act(WR, ("ps", 3584, 3840))
+    def late_constants(k):
+        if k == 2:
+            ts(full("xy"), full("j143"), C15, YW, OP.is_equal, OP.mult)
+            ts(full("xu"), full("j143"), C15, COF, OP.is_equal, OP.mult)
+        elif k == 0:
+            tt(IDM, ip, ij, OP.is_equal)
+            ts(full("ci"), full("j16"), PB, 976.0, OP.add, OP.mult)
+            ts(full("aid"), IDM, ALPHA, None, OP.mult)
+            ts(full("cj"), full("ci"), 65535, None, OP.bitwise_and)
+            ts(full("nad"), IDM, -ALPHA, None, OP.mult)
+            vcopy(full("cw"), full("cj"))
+            for h in range(2):
+                tt(half("b16", h, 8), ("pg", 0, 8), ("ij", 0, 8), OP.is_equal)
+            ts(full("cw0"), full("cj"), 1.0 / 16, None, OP.mult)
+            ts(full("nid"), IDM, -1.0, None, OP.mult)
+        else:
+            vset(full("tw"), 2.0)
+            vset(NH, -0.5)
+            vset(full("one"), 1.0)
+            vset(full("mon"), -1.0)
+            vscan(full("p2"), full("tw"), ("nh", 0, 16), 2.0 ** -22, OP.mult, OP.max)
+            ts(full("s8"), full("d8"), 0.0, None, OP.is_equal)
+            tt(full("e16"), pb, jb, OP.is_equal)
+            vset(full("eps"), -73.0 / 32)
+            tt(full("x8"), ip, jg, OP.is_equal)
+            tt(full("p8"), full("p2"), full("b16"), OP.mult)
+            for n, f in (("sid", 7.0 / 32), ("hid", 0.5), ("eid", 8.0)):
+                ts(full(n), IDM, f, None, OP.mult)
+            for h in range(2):
+                vsum(col("cf", h), half("p8", h, 8))
+            for h in range(2):
+                ts(sq("cm", h), full("e16"), col("cf", h), None, OP.mult)
 
-    def starts():
-        group(7, [mm(("ps", 3584, 3840), sq("tri"), WR, True, False),
-                  mm(("ps", 3584, 3840), sq("tru"), ("wr", 15, 271), False, True)])
-        group(7, [mm(("ps", 3840, 4096), sq("bo"), WR, True, True)])
-        vscan(full("st"), ("ps", 3584, 3840), full("lim"), OP.add, OP.min)
-        vcopy(full("stu"), full("st"))
+    oh = ["oh0", "oh1", "oh2", "oh0"]
 
-    def scatter():
-        op("V", lambda e: e.tensor_copy(T.win[:, 0:12288].indirect(T.stu[:, 0:256]), T.dif[:]),
-           [full("stu"), full("dif")], [full("win")])
-
-    def totals_t():
-        op("V", lambda e: e.tensor_reduce(T.sm[:, 0:1], ps[:, 3840:4096], AxisListType.X, OP.add), (), [("sm", 0, 1)], [7])
-        ts(("sm", 1, 2), ("sm", 0, 1), 8192.0, 0.5, OP.min, OP.mult)
-        ts(("si", 0, 1), ("sm", 1, 2), -0.25, None, OP.add)
-        ts(("t2", 0, 1), ("si", 0, 1), 1.0 / 2048, None, OP.mult)
-
-    def expand_seq():
-        vscan(full("ex"), ("win", 0, 8192), ("win", 0, 8192), OP.add, OP.max)
-
-    def expand_w():
-        for h in range(4):
-            o = (h % 3) * 1024
-            for b in range(4 * h, 4 * h + 4):
-                c = o + (b % 4) * 256
-                group(c // 512, [mm(("ps", c, c + 256), sq("xpd", b), WR, True, True)])
-            for b in range(4 * h, 4 * h + 4):
-                c = o + (b % 4) * 256
-                op("S", lambda e: e.activation(T.nat[:, b::16], ps[:, c:c + 256], AF.Copy), (), [("nat", b, b + 1)], [c // 512])
-
-    def hash_products(zr):
-        for kk in range(2):
-            o = 3584 + kk * 256
-            group(7, [mm(("ps", o, o + 256), sq("uhi"), zr, True, False), mm(("ps", o, o + 256), sq("ulo"), zr, False, kk == 0)]
-                  + ([mm(("ps", o, o + 256), sq("u128"), zr, False, True)] if kk else []))
-
-    mbuf = ("w0r", "ptx")
-
-    def members(place, t):
-        for m in MEMBERS.get((place, t), []):
-            gather("S", (mbuf[m], 0, 4096), full("nat"), half("lmu", t + m))
-
-    def member_sum(m, bank):
-        o = bank * 512 + 256 * m
-        group(bank, [mm(("ps", o, o + 256), sq("idm"), (mbuf[m], b, 4096, 16), b == 0, b == 15) for b in range(16)])
-
-    def member_light(m, bank):
-        o = bank * 512 + 256 * m
-        ts(half("lfl", m), ("ps", o, o + 256), 23.5, None, OP.is_lt)
-
-    wraps = []
-
-    def pieces(place, t):
-        for c, k in PIECES.get((place, t), []):
-            op("S", lambda e: e.activation(T.invw[:, 0:4096].indirect(T.lmu[:, c * 256 + 64 * k:c * 256 + 64 * k + 64]),
-                                           T.vals[:, k * 1024:(k + 1) * 1024], AF.Silu),
-               [full("lmu"), half("vals", k, 1024)], [full("invw")])
+    def tasks(place, t):
+        for task in TASKS.get((place, t), []):
+            if task[0] == "mem":
+                gather(task[1], full("mg%d" % task[2]), full("nat"), half("lmu", t + task[2]))
+                continue
+            q, c, k = task[1:]
+            w = "inv%d" % (c % 2)
+            o, v = T[w][:, 0:4096].indirect(T.lmu[:, c * 256 + 64 * k:c * 256 + 64 * k + 64]), T.vals[:, k * 1024:(k + 1) * 1024]
+            op(q, (lambda e: e.tensor_copy(o, v)) if q == "V" else (lambda e: e.activation(o, v, AF.Silu)),
+               [full("lmu"), half("vals", k, 1024)], [full(w)])
             if k == 3:
-                dma("G", T.rbf[:], T.invw[:], [full("invw")], [full("rbf")])
-                wraps.append(c)
+                dma("G", T[oh[c]][:], T[w][:], [full(w)], [full(oh[c])])
 
-    def inv_wrap(bank):
-        while wraps:
-            c = wraps.pop()
-            o = bank * 512
-            group(bank, [mm(("ps", o, o + 256), sq("edg", b), ("rbf", b, 4096, 16), b == 0, b == 15) for b in range(16)])
-            vcopy(full("ivi"), ("ps", o, o + 256))
-            vcopy(half("inv", c), full("ivi"))
+    def expand(t):
+        group(7, [mm(pr(3584, 256), full("bo"), WR)])
+        group(6, [mm(pr(3072, 256), full("tri"), WR)])
+        group(6, [mm(pr(3328, 16), sq("m16", b), ("wr", b, 256, 16), b == 0, b == 14) for b in range(15)])
+        X, Y = pr(2048, 272), pr(2560, 272)
+        vscan(("pre", 1, 257), pr(3584, 256), WR, 0.0, OP.add, OP.max)
+        ts(col("sm"), col("pre", 256), 8192.0, 0.5, OP.min, OP.mult)
+        tt(pr(2048, 256), pr(3072, 256), ("pre", 0, 256), OP.add)
+        ts(col("si"), col("sm"), -0.25, None, OP.add)
+        tt(pr(2304, 16), pr(3328, 16), ("pre", 0, 256, 16), OP.add)
+        ts(col("tau"), col("si"), 1.0 / 2048, None, OP.mult)
+        op("V", lambda e: e.reciprocal(ap(col("rr")), ap(col("tau"))), [col("tau")], [col("rr")])
+        ts(Y, X, col("rr"), MAGIC, OP.mult, OP.add)
+        ts(full("y0"), Y, -MAGIC, col("tau"), OP.add, OP.mult)
+        tt(full("ltf"), X, full("y0"), OP.is_gt)
+        tt(("cc", 1, 273), Y, full("ltf"), OP.add)
+        tt(full("jj"), ("cc", 1, 257), ("cc", 0, 256), OP.subtract)
+        tt(full("ar"), ("cc", 257, 273), full("lim"), OP.min)
+        ts(full("jf"), full("jj"), NZ, JK, OP.mult, OP.add)
+        ts(full("stu"), full("ar"), -MAGIC, None, OP.add)
+        op("V", lambda e: e.tensor_copy(T.win[:, 0:4352].indirect(T.stu[:, 0:16]), T.jf[:]), [full("stu"), full("jf")], [full("win")])
+        if t == 0:
+            late_constants(2)
+        zr = centres(t)[0]
+        group(7, [mm(pr(3584, 16), shifted("xu", b), (zr[0], zr[1] + b, zr[2], 16), b == 0, b == 15) for b in range(16)])
+        vscan(full("scn"), ("win", 0, 4096), ("win", 0, 4096), INI, OP.add, OP.max)
+        if t < 2:
+            clear_window()
+        if t == 0:
+            late_constants(0)
+        tasks("pre", t)
+        for k in range(4):
+            group(k, [mm(pr(512 * k, 64), shifted("xy", b), ("scn", 1024 * k + b, 1024 * k + 1024, 16), b == 0, b == 15) for b in range(16)])
+        for k in range(4):
+            ts(half("fu", k, 64), pr(512 * k, 64), 1919.0, None, OP.add)
+            if FQ[t][k] == "S":
+                gather("S", half("ff", k, 1024), full("ptx"), half("fu", k, 64))
+            for c in range(4 * k, 4 * k + 4):
+                ts(("hx", c, 512, 16), full("kap"), pr(3584 + c, 1), col("cw", c), OP.mult, OP.add, W=[col("hx", c)])
+        op("V", lambda e: e.tensor_scalar(T.hy[:], T.hx[:], 4, 4095, OP.arith_shift_right, OP.bitwise_and), [("hx", 0, 16)], [full("hy")])
+        for k in range(4):
+            if FQ[t][k] == "V":
+                gather("V", half("ff", k, 1024), full("ptx"), half("fu", k, 64))
+        vcopy(full("hu"), full("hy"))
 
-    for h, n in enumerate(("zs", "zh")):
-        vcopy(half("lmu", h, 512), full(n))
-    starts()
-    for c in range(8 - DV):
-        o = (c % 6) * 512
-        group(c % 6, [mm(("ps", o, o + 512), sq("idm"), ("ptx", c * 512 + 16, c * 512 + 528), True, False),
-                      mm(("ps", o, o + 512), sq("nid"), ("ptx", c * 512 + 15, c * 512 + 527), False, True)])
-        act(half("dif", c, 512), ("ps", o, o + 512))
-    tt(("dif", 4096 - 512 * DV, 4096), ("ptx", 4112 - 512 * DV, 4112), ("ptx", 4111 - 512 * DV, 4111), OP.subtract)
-    scatter()
-    pieces("setup", 0)
-    for b in range(16):
-        op("S", lambda e: e.activation(T.xpd[:, b * 128:b * 128 + 128], T.bo[:], AF.Copy, scale=T.colb[:, b:b + 1]),
-           [full("bo"), full("colb")], [sq("xpd", b)])
-    totals_t()
-    ci1, ci2, ci3, ci4 = [sq(n) for n in ("ci1", "ci2", "ci3", "ci4")]
-    ts(ci1, pb, 2.0, 1.0, OP.mult, OP.add)
-    ts(ci2, jb, 8.0, 7.0, OP.mult, OP.add)
-    ts(full("hx"), full("hx"), 65535, None, OP.bitwise_and)
-    tt(ci3, ci1, ci2, OP.mult)
-    ts(sq("aid"), sq("idm"), ALPHA, None, OP.mult)
-    ts(ci4, ci3, 65504, None, OP.bitwise_and)
-    ts(ci2, ci1, 128.0, None, OP.mult)
-    tt(sq("uhi"), ci4, sq("bo"), OP.mult)
-    ts(ci4, ci3, 31, None, OP.bitwise_and)
-    ts(sq("nad"), sq("idm"), -ALPHA, None, OP.mult)
-    tt(sq("ulo"), ci4, sq("bo"), OP.mult)
-    tt(sq("u128"), ci2, sq("bo"), OP.mult)
-    vcopy(full("cf"), full("hx"))
-    hash_products(("zin", 0, 256))
-    expand_seq()
-    iota("win", 0, 8192, [[0, 8192]], 0, 0)
-    expand_w()
+    def centres(t):
+        return [("zin", 0, 256), ("zrr", 0, 256), ("zrr", 256, 512)][t], half("zin", t + 1)
+
+    def natural(bank):
+        for h in range(2):
+            group(bank, [mm(pr(bank * 512 + 32 * k + 16 * h, 16), ("wr", h, 256, 2), half("idm", k, 16)) for k in range(8)])
+
+    tasks("setup", 0)
 
     for t in range(3):
         last = t == 2
-        zr = [("zin", 0, 256), ("zrr", 0, 256), ("zrr", 256, 512)][t]
-        zt = half("zin", t + 1)
-        pre = MEMBERS[("pre", t)]
-        late = [m for m in range(2) if m not in pre]
-        members("pre", t)
-        for n, z in (("zx0", zr), ("zx1", zt)):
-            for j in range(2):
-                op("S", lambda e: e.activation(T[n][:, j::2], ap(z), AF.Copy), [rng(z)], [(n, j, j + 1)])
-        for k in range(2):
-            tt(half("hx", k), ("ps", 3584 + 256 * k, 3840 + 256 * k), half("cf" if t == 0 else "ca", k), OP.add)
-        for k in range(2):
-            ts(half("hy", k), half("hx", k), 4, 4095, OP.arith_shift_right, OP.bitwise_and)
-        for k in range(2):
-            ts(half("hx", k), half("hy", k), ("t2", 0, 1), -4095.5 + 1.0 / 4096, OP.mult, OP.add)
-        for k in range(2):
-            ts(half("hu", k), half("hx", k), 4095.0, None, OP.add)
-        pieces("net", t)
-        for k in range(4):
-            gather(NETQ[t][k], half("net", k, 2048), full("ex"), half("hu", k, 128))
-        for m in pre:
-            member_sum(m, 6)
-        if t == 0:
-            tt(("b8", 0, 8), ("pg", 0, 8), ("ij", 0, 8), OP.is_equal)
-            ts(ci3, ip, 7, None, OP.bitwise_and)
+        zz = centres(t)
+        expand(t)
+        mine = list(zip(NETV[t], [k for k in range(8) if NETQ[t][k] == "V"]))
+        for k in range(8):
+            if NETQ[t][k] == "S":
+                gather("S", half("net", k, 1024), full("ff"), half("hu", k, 64))
+        tasks("net", t)
+        ts(full("w2x"), WR, 2.0, 8.0, OP.mult, OP.min)
 
-        nab, inds = [0], {}
+        slot, at = [0], {}
+        steps = [(s % 2, s // 2) for s in range(16)]
 
-        def differences(v):
-            e = (v // 8) * 4096 + 4096
-            for h in range(2):
-                o = (v % 3) * 1024 + h * 512
-                b0 = e - 4096 + (v // 2 % 4) * 2 + h
-                group(o // 512, [mm(("ps", o, o + 512), sq("nad"), full("zx%d" % (v % 2)), True, False),
-                                 mm(("ps", o, o + 512), sq("aid"), ("net", b0, e, 8), False, True)])
+        def pair():
+            slot[0] += 1
+            return slot[0] % 3 * 1024
 
-        def near(v):
-            i = half("ind", v % 6, 1024)
-            p = half("ps", v % 3, 1024)
-            if v in VUNITS[t]:
-                ts(i, p, 12582912.0, 12582912.0, OP.add, OP.is_equal)
-                return
-            a = half("ab", nab[0] % 4, 1024)
-            nab[0] += 1
-            act(a, p, AF.Abs)
-            ts(i, a, 0.5, None, OP.is_le)
+        def differences(s):
+            r, k = steps[s]
+            o = pair()
+            for c in (o, o + 512):
+                group(c // 512, [mm(pr(c, 512), full("aid"), half("net", 2 * k + c // 512 % 2, 512), True, False)]
+                      + [mm(pr(c + 256 * j, 256), full("nad"), zz[r], False, j == 1) for j in range(2)])
+            ts(half("ind", s % 6, 1024), pr(o, 1024), MAGIC, MAGIC, OP.add, OP.is_equal)
 
-        def counts(v):
-            r = v % 2
-            for h in range(2):
-                for lb in range(2):
-                    for j in range(2):
-                        c = (6 + r) * 512 + lb * 256 + ((v // 8) * 16 + (v // 2 % 4) * 2 + h + 8 * j) * 8
-                        i = (v % 6) * 1024 + h * 512 + lb * 256
-                        group(6 + r, [mm(("ps", c, c + 8), ("ind", i + j, i + 256, 2), ("b8", 0, 8), True, True)])
+        def counts(s):
+            r, k = steps[s]
+            group(6 + r, [mm(pr((6 + r) * 512 + lb * 256 + 4 * k + j, 256 - 4 * k - j, 32), sq("ind", s % 6 * 8 + 2 * j + lb), B8)
+                          for j in range(4) for lb in range(2)])
 
-        def scans(kk, which):
-            k, n, o0, o1 = ("kmx", "tmx", OP.min, OP.max) if which == 0 else ("kmn", "tmn", OP.max, OP.min)
-            for h in range(2):
-                vscan(half(n, h, 2048), full(k), half("net", 2 * kk + h, 2048), o0, o1)
-            if kk == 0:
-                vcopy(full("mn0" if which else "mx0"), (n, 15, 4096, 16))
-            elif which == 0:
-                tt(full("mxx"), full("mx0"), (n, 15, 4096, 16), OP.max)
-            else:
-                tt(full("mnn"), full("mn0"), (n, 15, 4096, 16), OP.min)
-
-        for s in range(16 + LAG):
-            if s < 16:
-                differences(s)
-                near(s)
-            members(s, t)
-            pieces(s, t)
-            if s == 1:
-                for m in pre:
-                    member_light(m, 6)
-            if s in WRAP[t]:
-                inv_wrap(6 if s < 2 else 3)
-            if s == LATE:
-                for m in late:
-                    member_sum(m, 2)
-            if s >= LAG:
-                counts(s - LAG)
-            if s == 0 and t == 0:
-                tt(sq("b2"), ci3, jg, OP.is_equal)
-                for b in range(16):
-                    ts(sq("edg", b), sq("idm"), ("colb", b, b + 1), None, OP.mult)
-            if s in SCANS:
-                scans(*SCANS[s])
-            if s == 12:
-                tt(full("ivi"), full("mxx"), full("mnn"), OP.add)
-                ts(full("yy"), full("ivi"), 1, None, OP.arith_shift_right)
-            if s == 16:
-                for m in late:
-                    member_light(m, 2)
-                for r, z in ((0, zr), (1, zt)):
-                    tt(half("zs", r), z, full("yy"), OP.add)
-                for r in range(2):
-                    ts(half("zh", r), half("zs", r), 1, None, OP.arith_shift_right)
-                for r, z in ((0, zr), (1, zt)):
-                    tt(half("zd", r), half("zh", r), z, OP.subtract)
-        for r in range(2):
-            ts(half("h01", r, 512), ("ps", (6 + r) * 512, (7 + r) * 512), 11.5, None, OP.is_ge)
-        for r in range(2):
+        def member_sums(m):
+            o = pair()
             for lb in range(2):
-                c = 2048 + r * 256 + lb * 128
-                group(4, [mm(("ps", c, c + 128), sq("h01", r * 4 + lb * 2 + k), sq("idm"), k == 0, k == 1) for k in range(2)])
-        vcopy(full("hts"), ("ps", 2048, 2560))
-        group(5, [mm(("ps", 2560, 3072), sq("b2"), full("hts"), True, True)])
-        s0, s1, l0, l1 = half("sel", 0), half("sel", 1), half("lg", 0), half("lg", 1)
-        ts(s0, ("ps", 2560, 2816), 0.5, None, OP.is_lt)
-        ts(full("m1"), ("ps", 2816, 3072), 0.5, None, OP.is_lt)
-        tt(l0, s0, half("lfl", 0), OP.mult)
-        tt(s1, full("m1"), s0, OP.is_gt)
-        tt(l1, s1, half("lfl", 1), OP.mult)
-        for k in range(4):
-            gather("S", half("w0r", k, 1024), l0, half("inv", t * 4 + k, 64))
-            gather("V", half("ptx", k, 1024), l1, half("inv", t * 4 + 4 + k, 64))
-        for k in range(4):
-            c = 3072 + 64 * k
-            group(6, [mm(("ps", c, c + 64), sq("edg", b), (mbuf[m], k * 1024 + b, k * 1024 + 1024, 16), b == 0 and m == 0, b == 15 and m == 1)
-                      for m in range(2) for b in range(16)])
-        for k, (x, f) in enumerate(((s0, 1.0), (s1, 1.0), (l0, -1.0), (l1, -1.0))):
-            op("S", lambda e: e.activation(T.h01[:, k * 256:k * 256 + 256], ap(x), AF.Identity, scale=f, accum_out=T.acc[:, k:k + 1]),
-               [x], [half("h01", k), ("acc", k, k + 1)])
-        pieces("marks", t)
+                group(o // 512, [mm(pr(o + 8 * lb, 8), ("mg%d" % m, 2048 * lb + b, 2048 * lb + 2048, 16), ("s8", 0, 8), b == 0, b == 15)
+                                 for b in range(16)])
+            ts(half("lth", m, 16), pr(o, 16), 23.5, None, OP.is_lt)
+
+        def largest(r):
+            vscan(half("cmx", r, 512), full("kmx"), pr((6 + r) * 512, 512), 0.0, OP.min, OP.max)
+
+        def words(r):
+            o = (6 + r) * 512
+            group(6 + r, [mm(pr(o + 8 * lb, 8), sq("cm", lb), half("fh", 2 * r + lb, 8)) for lb in range(2)])
+            tt(half("wd", r, 16), pr(o, 16), full("b16"), OP.mult)
+
+        def lookups(r):
+            o = (6 + r) * 512
+            group(6 + r, [mm(pr(o, 512), full("sid"), full("eps"), True, False)]
+                  + [mm(pr(o + 256 * h + a, 256 - a, 16), (oh[t + r], 2048 * h + a, 2048 * h + 2048, 16), half("wd", r, 16), False, h == 1 and a == 15)
+                     for h in range(2) for a in range(16)])
+
+        def marks(r):
+            x = pr((6 + r) * 512, 512)
+            ts(full("qq"), x, MAGIC, -MAGIC, OP.add, OP.add)
+            tt(half("bt", r, 512), x, full("qq"), OP.is_gt)
+
+        order = list(range(13)) + [14, 13, 15]
+        top = [("cmx", 512 * r + 31, 512 * r + 512, 32) for r in range(2)]
+        for n in range(16 + LAG):
+            for at_step, k in mine:
+                if at_step == n:
+                    gather("V", half("net", k, 1024), full("ff"), half("hu", k, 64))
+            if n == mine[-1][0]:
+                fold(t)
+            if n == 0 and t == 0:
+                late_constants(1)
+            for m in range(2):
+                if SUMS[t][m] == n:
+                    member_sums(m)
+            if n < 16:
+                differences(order[n])
+            if n >= LAG:
+                counts(order[n - LAG])
+                if order[n - LAG] == 14:
+                    largest(0)
+                    ts(half("selh", 0, 16), top[0], 11.5, None, OP.is_lt)
+                    ts(full("nsl"), top[0], 11.5, None, OP.is_ge)
+                    tt(half("fh", 0, 16), half("selh", 0, 16), half("lth", 0, 16), OP.min)
+            tasks(n, t)
+        largest(1)
+        tt(full("inn"), full("nsl"), half("lth", 1, 16), OP.min)
+        ts(full("tw"), top[1], 11.5, None, OP.is_lt)
+        words(0)
+        tt(half("fh", 1, 16), full("tw"), full("inn"), OP.min)
+        tt(half("selh", 1, 16), full("tw"), full("nsl"), OP.min)
+        lookups(0)
+        words(1)
         for r in range(2):
-            tt(half("zm", r), half("sel", r), half("zd", r), OP.mult)
-        for r, z in ((0, zr), (1, zt)):
+            group(r, [mm(pr(512 * r + 128 * lb, 128), half("selh", 2 * r + lb, 8), IDM, m=8) for lb in range(2)])
+            act(half("st8", r), pr(512 * r, 256), parts=8)
+        lookups(1)
+        marks(0)
+        mx, mn = half("mm", 2 * t), half("mm", 2 * t + 1)
+        group(2, [mm(pr(1024, 256), full("hid"), mx, True, False), mm(pr(1024, 256), full("hid"), mn, False, False),
+                  mm(pr(1024, 256), full("hid"), NH, False, True)])
+        group(3, [mm(pr(1536, 8), full(n), half(b, k, 8), (n, k) == ("one", 0), (n, k) == ("mon", 3))
+                  for n, b in (("one", "selh"), ("mon", "fh")) for k in range(4)])
+        marks(1)
+        tasks("tail", t)
+        group(4, [mm(pr(2048, 256), IDM, WR, True, False)]
+              + [mm(pr(2048 + 128 * (k // 2 % 2), 128), sq("bt", k), full("eid"), False, k == 7) for k in range(8)])
+        ts(full("yy"), pr(1024, 256), MAGIC, -MAGIC, OP.add, OP.add)
+        for r in range(2):
+            group(r, [mm(pr(512 * r, 256), full("x8"), half("st8", r), k=8)])
+        tt(full("w1"), pr(2048, 256), full("w2x"), OP.min)
+        group(5, [mm(pr(2560, 256), full("bo"), full("w1"))])
+        for r in (1, 0):
+            group(2, [mm(pr(1024 + 256 * r, 256), IDM, full("yy"), True, False), mm(pr(1024 + 256 * r, 256), full("nid"), zz[r], False, True)])
+        act(full("yz2"), pr(1024, 512))
+        tt(("a8", 0, 8), pr(1536, 8), B8, OP.mult)
+        vsum(col("sm", 2), pr(2560, 256))
+        vsum(col("yat", t), ("a8", 0, 8))
+        ts(col("sc"), col("sm", 2), 7168.5, 0.5, OP.is_le, OP.max)
+        if not last:
+            ts(full("cw"), full("cw0"), col("yat", t), 16.0, OP.add, OP.mult)
+        ts(full("w2"), full("w1"), col("sc"), 128.25, OP.mult, OP.add)
+        tt(half("ee", 1), pr(512, 256), half("yz2", 1), OP.mult)
+        ts(WR, full("w2"), -128.0, None, OP.add)
+
+        def centre(r):
             o = half("znew", 2 * t + r)
-            tt(o, half("zm", r), z, OP.add)
+            group(r, [mm(pr(512 * r + 256, 256), IDM, zz[r], True, False), mm(pr(512 * r + 256, 256), full("hid"), half("ee", r), False, False),
+                      mm(pr(512 * r + 256, 256), full("hid"), NH, False, True)])
+            ts(o, pr(512 * r + 256, 256), MAGIC, -MAGIC, OP.add, OP.add)
             if r == 0:
                 send(rank + 1 + t, ap(half("fin", t)), ap(o), "af%d" % t, [o])
             elif not last:
                 send(rank - 1, ap(half("zrr", t)), ap(o), "ar%d" % (t + 1), [o])
             else:
                 send(rank - 1, ap(half("fin", 3)), ap(o), "af3", [o])
-        ts(full("wf"), ("ps", 3072, 3328), 0.5, 1.0, OP.is_ge, OP.add)
-        tt(full("wt"), WR, full("wf"), OP.mult)
-        ts(full("w1"), full("wt"), 8.0, None, OP.min)
-        group(3, [mm(("ps", 1536, 1792), sq("bo"), full("w1"), True, True)])
-        op("V", lambda e: e.tensor_reduce(T.sm[:, 2:3], ps[:, 1536:1792], AxisListType.X, OP.add), (), [("sm", 2, 3)], [3])
-        ts(("hv", 0, 1), ("sm", 2, 3), 7168.5, -0.5, OP.is_gt, OP.mult)
-        ts(("sc", 0, 1), ("hv", 0, 1), 1.0, None, OP.add)
-        ts(("bi", 0, 1), ("hv", 0, 1), -0.5, 128.0, OP.mult, OP.add)
-        ts(full("w2"), full("w1"), ("sc", 0, 1), ("bi", 0, 1), OP.mult, OP.add)
-        ts(WR, full("w2"), -128.0, None, OP.add)
-        if not last:
-            starts()
-            scatter()
-            totals_t()
-            expand_w()
-            hash_products(half("zrr", t))
-        op("V", lambda e: e.tensor_reduce(T.yat[:, t:t + 1], T.acc[:, 0:4], AxisListType.X, OP.add), [("acc", 0, 4)], [("yat", t, t + 1)])
-        if not last:
-            ts(("a16", 0, 1), ("yat", t, t + 1), 16.0, None, OP.mult)
-            ts(full("ca"), full("cf"), ("a16", 0, 1), None, OP.add)
-            expand_seq()
-            if t == 0:
-                iota("win", 0, 8192, [[0, 8192]], 0, 0)
 
+        tt(half("ee", 0), pr(0, 256), half("yz2", 0), OP.mult)
+        centre(1)
+        natural(3)
+        centre(0)
+        if not last:
+            act(full("wt"), pr(1536, 256))
+            dmas("Y", [(T.nat[16 * k:16 * k + 1, :], ap(half("wt", k, 32))) for k in range(8)], [full("wt")], [full("nat")])
+            dma("Y", ap(("yz", t * 256, t * 256 + 256)), ap(half("fin", t)), [half("fin", t)])
+            tasks("post", t)
+
+    act(full("wo"), pr(1536, 256))
+    for q, ks in (("S", (0, 1, 2, 3)), ("Y", (4, 5, 6, 7))):
+        dmas(q, [(T.yw[k:k + 1, :], ap(half("wo", k, 32))) for k in ks], [full("wo")])
     dma("Y", T.ya[:, :], T.yat[0:128:16, 0:3], [("yat", 0, 3)])
-    for h in range(4):
-        o = (h % 3) * 1024
-        for b in range(4 * h, 4 * h + 4):
-            c = o + (b % 4) * 256
-            group(c // 512, [(ps[0:8, c:c + 256], T.xpd[:, b * 128:b * 128 + 128:16], T.wr[:, 16:272], True, True, [sq("xpd", b), WR])])
-        for b in range(4 * h, 4 * h + 4):
-            c = o + (b % 4) * 256
-            if b % 4 < 2:
-                op("S", lambda e: e.activation(T.vals[0:8, b::16], ps[0:8, c:c + 256], AF.Copy), (), [("vals", b, b + 1)], [c // 512])
-            else:
-                op("V", lambda e: e.tensor_copy(T.vals[0:8, b::16], ps[0:8, c:c + 256]), (), [("vals", b, b + 1)], [c // 512])
-    dma("Y", T.yw[:, :], T.vals[0:8, :], [full("vals")])
-    for c in range(4):
-        dma("Y", ap(("yz", c * 256, c * 256 + 256)), ap(half("fin", c)), [half("fin", c)])
+    dma("Y", ap(("yz", 512, 1024)), ap(("fin", 512, 1024)), [("fin", 512, 1024)])
     for s, v in totals.items():
         if known["G"].get(s, 0) < v:
             g.wait_ge(T.sem[s], v)

from concourse.bass import DstId, RemoteDMATransfer
from concourse.mybir import AluOpType, AxisListType, ActivationFunctionType

OP = AluOpType
AF = ActivationFunctionType
ALPHA = 226.0 / 32768.0
MAGIC = 12582912.0
BASE = 65536.0 + 255.5

TASKS = {("setup", 0): [("inv", "S", c, k) for c in range(2) for k in range(4)],
         ("net", 0): [("mem", "S", 0), ("mem", "S", 1)], ("net", 1): [("mem", "S", 0), ("mem", "S", 1)], ("net", 2): [("mem", "S", 0), ("mem", "S", 1)],
         ("tail", 0): [("inv", "S", 2, 0), ("inv", "S", 2, 1)], ("post", 0): [("inv", "S", 2, 2), ("inv", "S", 2, 3)],
         ("tail", 1): [("inv", "S", 3, 0), ("inv", "S", 3, 1)], ("post", 1): [("inv", "S", 3, 2), ("inv", "S", 3, 3)]}
FQ = ["VVVV", "SSSV", "SSSV"]
NETQ = ["VVVVSSSS", "SVSSSSSS", "SVSSSSSS"]
NETV = [[0, 0, 1, 3], [0], [0]]
SUMS = {0: {0: 13, 1: 16}, 1: {0: 13, 1: 16}, 2: {0: 13, 1: 16}}
LAG = 2
NSEND = 8
NFOLD = 8


def _table():
    out = {"ps": ("psum", [128, 4096], "float32")}
    for d, cols in (("bfloat16", "ptx:4096 win:4352 dfl:1088 scn:4096 ff:4096 net:8192 ind:6144 nat:4096 mg0:4096 mg1:4096 oh0:4096 oh1:4096"
                     " oh2:4096 zo:1024 zin:1024 zrr:512 fin:1024 znew:1536 hb:1536 mm:1536 m16:2048 idm:128 nid:128 hid:128 eid:128"
                     " aid:128 nad:128 bo:128 lt:128 tri:128 key:128 one:128 mon:128 e16:128 cm:256 x8:128 xs:144 xu:144 xy:144 b16:16 s8:16"
                     " kap:32 kmx:512 nh:256 dd:256 wr:256 w1:256 w2:256 w2x:256 jj:256 jf:256 cmx:1024 selh:32 lth:32 fh:32 nsl:16"
                     " inn:16 wd:32 bt:1024 st8:512 yy:256 yz2:512 ee:512 wt:256 tw:16 eps:512 sid:128 dz:256"),
                    ("float32", "inv0:4096 inv1:4096 vals:4096 pre:272 y0:272 ltf:272 cc:288 qq:512 lim:16 col:16 sm:16 tau:16 rr:16 sc:16"
                     " a8:16 ar:16 yat:16 cw0:16 cw:16 p2:16 p8:16 cf:16 wo:256 j143:144"),
                    ("int32", "ip:128 ij:128 pg:128 pb:128 jg:128 jb:128 dw:144 d8:16 j16:16 jd:256 si:16 ci:16 cj:16 hx:512 hy:512 lmi:1024"),
                    ("uint16", "lmu:1024 stu:16 fu:256 hu:512")):
        for c in cols.split():
            n, w = c.split(":")
            out[n] = ("sbuf", [128, int(w)], d)
    return out


SCRATCH = _table()
INTS = [n for n in SCRATCH if SCRATCH[n][2] == "int32"]
NDMA = 40
SEMAPHORES = (["qv", "qs", "qp", "qg", "sent", "az01", "az2", "az3", "ar1", "ar2", "af0", "af1", "af2", "af3"]
              + ["%s%d" % (n, t) for n in ("fo", "hf", "am") for t in range(3)] + ["d%d" % k for k in range(NDMA)])
QSEM = {"V": "qv", "S": "qs", "P": "qp", "G": "qg"}


def helpers(cores, topo):
    out = []
    for c in cores:
        out.append([h for h in topo.cores_of(c) if topo.die(h) == topo.die(c) and h not in cores and h not in out][0])
    return out


def bits(engines):
    m = 0
    for e in engines:
        m |= 1 << e
    return m


def rank_program(g, core, T, topo):
    rank = T.rank_of(core)
    hands = helpers(list(T.cores), topo)
    if rank is None:
        if core in hands:
            dst = T.cores[hands.index(core)]
            rid, pid = topo.addr(dst)[:2]
            for t in range(3):
                g.wait_ge(T.sem["hf%d" % t], 2 * NFOLD)
                g.remote_dma(T.mm[:, 512 * t:512 * t + 512], T.hb[:, 512 * t:512 * t + 512], T.sem["am%d" % t], T.sem.sent, pid, rid,
                             bits(topo.engines(core, dst)[:NSEND]))
            g.wait_ge(T.sem.sent, 3 * NSEND)
        return
    eng = {"V": g.vector, "S": g.scalar, "P": g.tensor, "G": g, "Y": g.sync}
    known = {q: {} for q in eng}
    count = {q: 0 for q in eng}
    recs, banks, totals, ndma = {}, {}, {}, [0]
    ps = T.ps

    def wait(q, toks):
        for s, v, ck in sorted(toks, key=lambda k: -sum(k[2].values())):
            if known[q].get(s, 0) < v:
                eng[q].wait_ge(T.sem[s], v)
            for s2, v2 in ck.items():
                if known[q].get(s2, 0) < v2:
                    known[q][s2] = v2

    def deps(q, R, W, B):
        toks = []
        for n, lo, hi in R:
            toks += [r[3] for r in recs.get(n, []) if r[2] == "w" and r[0] < hi and lo < r[1]]
        for n, lo, hi in W:
            toks += [r[3] for r in recs.get(n, []) if r[0] < hi and lo < r[1]]
        for b in B:
            toks += [tk for q2, tk in banks.get(b, {}).items() if q2 != q]
        return toks

    def note(q, tok, R, W, B):
        for n, lo, hi in W:
            recs[n] = [r for r in recs.get(n, []) if not (lo <= r[0] and r[1] <= hi)] + [(lo, hi, "w", tok, q)]
        for n, lo, hi in R:
            recs[n] = [r for r in recs.get(n, []) if not (r[2] == "r" and r[4] == q and lo <= r[0] and r[1] <= hi)] + [(lo, hi, "r", tok, q)]
        for b in B:
            banks.setdefault(b, {})
            banks[b][q] = tok

    def token(q, s, v):
        ck = dict(known[q])
        ck[s] = v
        totals[s] = v
        return (s, v, ck)

    def op(q, fn, R=(), W=(), B=()):
        wait(q, deps(q, R, W, B))
        count[q] += 1
        fn(eng[q]).then_inc(T.sem[QSEM[q]], 1)
        note(q, token(q, QSEM[q], count[q]), R, W, B)

    def group(bank, mats):
        for k, (o, l, r, a, b, R) in enumerate(mats):
            wait("P", deps("P", R, (), (bank,) if k == 0 else ()))
        for o, l, r, a, b, R in mats:
            ins = g.tensor.matmul(o, l, r, a, b)
        count["P"] += 1
        ins.then_inc(T.sem.qp, 1)
        tok = token("P", "qp", count["P"])
        for o, l, r, a, b, R in mats:
            note("P", tok, R, (), (bank,))

    def dmas(q, pairs, R=(), W=()):
        wait(q, deps(q, R, W, ()))
        s = "d%d" % ndma[0]
        ndma[0] += 1
        for out, in_ in pairs:
            eng[q].dma_start(out, in_).then_inc(T.sem[s], 16)
        note(q + s, token(q, s, 16 * len(pairs)), R, W, ())

    def dma(q, out, in_, R=(), W=()):
        dmas(q, [(out, in_)], R, W)

    def send(to, out, in_, sem, R):
        dst = T.cores[to % len(T.cores)]
        wait("G", deps("G", R, (), ()))
        rid, pid = topo.addr(dst)[:2]
        g.remote_dma(out, in_, T.sem[sem], T.sem.sent, pid, rid, bits(topo.engines(core, dst)[:NSEND]))
        totals["sent"] = totals.get("sent", 0) + NSEND

    def fold(t):
        dst = hands[rank]
        wait("G", deps("G", [full("net")], (), ()))
        rid, pid = topo.addr(dst)[:2]
        en = topo.engines(core, dst)
        g.remote_dma_fused([RemoteDMATransfer(dst_ids=[DstId(rid=rid, pnc=pid)], dma_engine_mask=bits(en[h * NFOLD:h * NFOLD + NFOLD]),
                                              remote_sem=T.sem["hf%d" % t], srcs=[T.net[:, k * 256:k * 256 + 256] for k in range(32)],
                                              dsts=[T.hb[:, 512 * t + 256 * h:512 * t + 256 * h + 256]], alu_op=2 + h) for h in range(2)],
                           local_sem=T.sem["fo%d" % t])
        note("fold", token("G", "fo%d" % t, 2 * NFOLD), [full("net")], (), ())

    def arrive(sem, name, lo, hi):
        totals[sem] = NSEND
        recs.setdefault(name, []).append((lo, hi, "w", (sem, NSEND, {sem: NSEND}), "net"))

    def full(n):
        return (n, 0, SCRATCH[n][1][1])

    def half(n, k, w=256):
        return (n, k * w, k * w + w)

    def sq(n, b=0):
        return (n, b * 128, b * 128 + 128)

    def col(n, c=0):
        return (n, c, c + 1)

    def pr(lo, w, step=None):
        return ("ps", lo, lo + w) if step is None else ("ps", lo, lo + w, step)

    def ap(x, parts=128):
        n, lo, hi = x[0], x[1], x[2]
        return T[n][0:parts, lo:hi:x[3]] if len(x) > 3 else T[n][0:parts, lo:hi]

    def rng(x):
        return (x[0], x[1], x[2])

    def bk(*xs):
        return [b for x in xs if x[0] == "ps" for b in range(x[1] // 512, (x[2] - 1) // 512 + 1)]

    def split(rs):
        return [rng(x) for x in rs]

    def tt(out, a, b, o):
        op("V", lambda e: e.tensor_tensor(ap(out), ap(a), ap(b), o), split((a, b)), split((out,)), bk(out, a, b))

    def ts(out, a, s1, s2, o0, o1=None, W=None, parts=128):
        c1 = ap(s1, parts) if isinstance(s1, tuple) else s1
        c2 = ap(s2, parts) if isinstance(s2, tuple) else s2
        R = [a] + [s for s in (s1, s2) if isinstance(s, tuple)]
        args = (c1, None, o0) if o1 is None else (c1, c2, o0, o1)
        op("V", lambda e: e.tensor_scalar(ap(out, parts), ap(a, parts), *args), split(R), W or split((out,)), bk(out, *R))

    def vcopy(out, a):
        op("V", lambda e: e.tensor_copy(ap(out), ap(a)), split((a,)), split((out,)), bk(out, a))

    def vset(out, c):
        op("V", lambda e: e.memset(ap(out), c), (), split((out,)))

    def act(out, a, func=AF.Copy, parts=128, **kw):
        op("S", lambda e: e.activation(ap(out, parts), ap(a, parts), func, **kw), split((a,)), split((out,)), bk(out, a))

    def vscan(out, a, b, init, o0, o1):
        R = [a, b] + ([init] if isinstance(init, tuple) else [])
        op("V", lambda e: e.tensor_tensor_scan(ap(out), ap(a), ap(b), ap(init) if isinstance(init, tuple) else init, o0, o1),
           split(R), split((out,)), bk(out, a, b))

    def vsum(out, a):
        op("V", lambda e: e.tensor_reduce(ap(out), ap(a), AxisListType.X, OP.add), split((a,)), split((out,)), bk(out, a))

    def gather(q, out, wn, off):
        w, o = ap(wn), ap(off)
        if q == "V":
            op("V", lambda e: e.tensor_copy(ap(out), w.indirect(o)), [wn, off], [rng(out)])
        else:
            op("S", lambda e: e.activation(ap(out), w.indirect(o), AF.Copy), [wn, off], [rng(out)])

    def mm(out, lhs, rhs, start=True, stop=True, k=128, m=128):
        return (ap(out, m), ap(lhs, k), ap(rhs, k), start, stop, [rng(lhs), rng(rhs)])

    def iota(n, pattern, base, cm):
        w = {} if n in INTS else {"allow_small_or_imprecise_dtypes": True}
        op("G", lambda e: e.iota(T[n][:], pattern, base, cm, **w), (), [full(n)])

    def shifted(n, b):
        return (n, 15 - b, 143 - b)

    WR, IDM, NH, B8 = full("wr"), full("idm"), full("nh"), ("b16", 0, 8)
    PB, C15, ISZ, NZ, JK, DEF, YW, INI, COF = [col("col", k) for k in range(9)]

    dma("Y", T.mg0[0:8, :], T.w0[:, :], (), [full("mg0")])
    dma("Y", T.zo[:], T.z0[:], (), [full("zo")])
    dma("S", T.lmi[:], T.lm[:], (), [full("lmi")])
    dma("S", T.ptx[:], T.pt[:], (), [full("ptx")])
    for a in (("az01", "zin", 0, 512), ("az2", "zin", 512, 768), ("az3", "zin", 768, 1024), ("ar1", "zrr", 0, 256), ("ar2", "zrr", 256, 512),
              ("af0", "fin", 0, 256), ("af1", "fin", 256, 512), ("af2", "fin", 512, 768), ("af3", "fin", 768, 1024),
              ("am0", "mm", 0, 512), ("am1", "mm", 512, 1024), ("am2", "mm", 1024, 1536)):
        arrive(*a)

    iota("ip", [[0, 128]], 0, 1)
    iota("jd", [[1, 16], [0, 16]], 0, 0)
    iota("dw", [[1, 144]], -15, -16)
    iota("ij", [[1, 128]], 0, 0)
    iota("j16", [[16, 16]], 0, 0)
    iota("j143", [[1, 144]], 0, 0)
    send(rank - 1, T.zin[:, 0:512], T.zo[:, 0:512], "az01", [full("zo")])
    iota("kap", [[8, 32]], 7, 0)
    iota("d8", [[-16, 16]], 0, 1)
    iota("nat", [[0, 4096]], 0, 0)
    send(rank - 2, T.zin[:, 512:768], T.zo[:, 512:768], "az2", [full("zo")])
    send(rank - 3, T.zin[:, 768:1024], T.zo[:, 768:1024], "az3", [full("zo")])
    iota("kmx", [[0, 16], [16, 32]], 0, 0)

    ip, ij, pg, pb, jg, jb = [sq(n) for n in ("ip", "ij", "pg", "pb", "jg", "jb")]
    vset(full("dfl"), 0.0)
    vset(col("pre"), 0.0)
    vset(col("cc"), MAGIC)
    ts(pb, ip, 15, None, OP.bitwise_and)
    ts(pg, ip, 4, None, OP.arith_shift_right)
    vcopy(PB, col("pb"))
    ts(full("xs"), full("dw"), 0.0, None, OP.is_equal, parts=8)
    ts(full("dd"), full("jd"), PB, None, OP.is_equal)
    ts(ISZ, PB, 0.0, None, OP.is_equal)
    ts(DEF, ISZ, -1.0, None, OP.add)
    ts(full("dfl"), full("dfl"), DEF, None, OP.add)

    def clear_window():
        dmas("Y", [(ap(half("win", k, 1088)), T.dfl[:]) for k in range(4)], [full("dfl")], [full("win")])

    clear_window()
    dma("Y", T.nat[0:128:16, :], T.w0[:, :], (), [full("nat")])
    for l in range(16):
        act(half("vals", l), full("dd"), scale=float(2 ** (20 - l)))
    group(7, [mm(pr(3584, 256), shifted("xs", b), ("mg0", b, 4096, 16), b == 0, b == 15, k=8) for b in range(16)])
    ts(jg, ij, 4, None, OP.arith_shift_right)
    ts(jb, ij, 15, None, OP.bitwise_and)
    ts(NZ, ISZ, -1.0, 1.0, OP.mult, OP.add)
    tt(full("bo"), pg, jg, OP.is_equal)
    tt(full("lt"), ip, ij, OP.is_lt)
    ts(JK, ISZ, 2.0, -1.0, OP.mult, OP.add)
    tt(full("key"), full("bo"), jb, OP.mult)
    vcopy(full("lmu"), full("lmi"))
    tt(full("tri"), full("lt"), full("bo"), OP.mult)
    for b in range(15):
        ts(sq("m16", b), full("key"), float(b), None, OP.is_gt)
        if b == 7:
            vcopy(WR, pr(3584, 256))
    ts(full("lim"), full("j16"), PB, MAGIC + 4096.0, OP.add, OP.add)
    ts(C15, col("pg"), 16.0, 15.0, OP.mult, OP.add)
    ts(YW, ISZ, 16.0 + 1.0 / 512, -1.0 / 512, OP.mult, OP.add)
    ts(INI, NZ, BASE + 1.0, None, OP.mult)
    ts(COF, PB, 2.0, 1.0, OP.mult, OP.add)

    def late_constants(k):
        if k == 2:
            ts(full("xy"), full("j143"), C15, YW, OP.is_equal, OP.mult)
            ts(full("xu"), full("j143"), C15, COF, OP.is_equal, OP.mult)
        elif k == 0:
            tt(IDM, ip, ij, OP.is_equal)
            ts(full("ci"), full("j16"), PB, 976.0, OP.add, OP.mult)
            ts(full("aid"), IDM, ALPHA, None, OP.mult)
            ts(full("cj"), full("ci"), 65535, None, OP.bitwise_and)
            ts(full("nad"), IDM, -ALPHA, None, OP.mult)
            vcopy(full("cw"), full("cj"))
            for h in range(2):
                tt(half("b16", h, 8), ("pg", 0, 8), ("ij", 0, 8), OP.is_equal)
            ts(full("cw0"), full("cj"), 1.0 / 16, None, OP.mult)
            ts(full("nid"), IDM, -1.0, None, OP.mult)
        else:
            vset(full("tw"), 2.0)
            vset(NH, -0.5)
            vset(full("one"), 1.0)
            vset(full("mon"), -1.0)
            vscan(full("p2"), full("tw"), ("nh", 0, 16), 2.0 ** -22, OP.mult, OP.max)
            ts(full("s8"), full("d8"), 0.0, None, OP.is_equal)
            tt(full("e16"), pb, jb, OP.is_equal)
            vset(full("eps"), -73.0 / 32)
            tt(full("x8"), ip, jg, OP.is_equal)
            tt(full("p8"), full("p2"), full("b16"), OP.mult)
            for n, f in (("sid", 7.0 / 32), ("hid", 0.5), ("eid", 8.0)):
                ts(full(n), IDM, f, None, OP.mult)
            for h in range(2):
                vsum(col("cf", h), half("p8", h, 8))
            for h in range(2):
                ts(sq("cm", h), full("e16"), col("cf", h), None, OP.mult)

    oh = ["oh0", "oh1", "oh2", "oh0"]

    def tasks(place, t):
        for task in TASKS.get((place, t), []):
            if task[0] == "mem":
                gather(task[1], full("mg%d" % task[2]), full("nat"), half("lmu", t + task[2]))
                continue
            q, c, k = task[1:]
            w = "inv%d" % (c % 2)
            o, v = T[w][:, 0:4096].indirect(T.lmu[:, c * 256 + 64 * k:c * 256 + 64 * k + 64]), T.vals[:, k * 1024:(k + 1) * 1024]
            op(q, (lambda e: e.tensor_copy(o, v)) if q == "V" else (lambda e: e.activation(o, v, AF.Silu)),
               [full("lmu"), half("vals", k, 1024)], [full(w)])
            if k == 3:
                dma("G", T[oh[c]][:], T[w][:], [full(w)], [full(oh[c])])

    def expand(t):
        group(7, [mm(pr(3584, 256), full("bo"), WR)])
        group(6, [mm(pr(3072, 256), full("tri"), WR)])
        group(6, [mm(pr(3328, 16), sq("m16", b), ("wr", b, 256, 16), b == 0, b == 14) for b in range(15)])
        X, Y = pr(2048, 272), pr(2560, 272)
        vscan(("pre", 1, 257), pr(3584, 256), WR, 0.0, OP.add, OP.max)
        ts(col("sm"), col("pre", 256), 8192.0, 0.5, OP.min, OP.mult)
        tt(pr(2048, 256), pr(3072, 256), ("pre", 0, 256), OP.add)
        ts(col("si"), col("sm"), -0.25, None, OP.add)
        tt(pr(2304, 16), pr(3328, 16), ("pre", 0, 256, 16), OP.add)
        ts(col("tau"), col("si"), 1.0 / 2048, None, OP.mult)
        op("V", lambda e: e.reciprocal(ap(col("rr")), ap(col("tau"))), [col("tau")], [col("rr")])
        ts(Y, X, col("rr"), MAGIC, OP.mult, OP.add)
        ts(full("y0"), Y, -MAGIC, col("tau"), OP.add, OP.mult)
        tt(full("ltf"), X, full("y0"), OP.is_gt)
        tt(("cc", 1, 273), Y, full("ltf"), OP.add)
        tt(full("jj"), ("cc", 1, 257), ("cc", 0, 256), OP.subtract)
        tt(full("ar"), ("cc", 257, 273), full("lim"), OP.min)
        ts(full("jf"), full("jj"), NZ, JK, OP.mult, OP.add)
        ts(full("stu"), full("ar"), -MAGIC, None, OP.add)
        op("V", lambda e: e.tensor_copy(T.win[:, 0:4352].indirect(T.stu[:, 0:16]), T.jf[:]), [full("stu"), full("jf")], [full("win")])
        if t == 0:
            late_constants(2)
        zr = centres(t)[0]
        group(7, [mm(pr(3584, 16), shifted("xu", b), (zr[0], zr[1] + b, zr[2], 16), b == 0, b == 15) for b in range(16)])
        vscan(full("scn"), ("win", 0, 4096), ("win", 0, 4096), INI, OP.add, OP.max)
        if t < 2:
            clear_window()
        if t == 0:
            late_constants(0)
        tasks("pre", t)
        for k in range(4):
            group(k, [mm(pr(512 * k, 64), shifted("xy", b), ("scn", 1024 * k + b, 1024 * k + 1024, 16), b == 0, b == 15) for b in range(16)])
        for k in range(4):
            ts(half("fu", k, 64), pr(512 * k, 64), 1919.0, None, OP.add)
            if FQ[t][k] == "S":
                gather("S", half("ff", k, 1024), full("ptx"), half("fu", k, 64))
            for c in range(4 * k, 4 * k + 4):
                ts(("hx", c, 512, 16), full("kap"), pr(3584 + c, 1), col("cw", c), OP.mult, OP.add, W=[col("hx", c)])
        op("V", lambda e: e.tensor_scalar(T.hy[:], T.hx[:], 4, 4095, OP.arith_shift_right, OP.bitwise_and), [("hx", 0, 16)], [full("hy")])
        for k in range(4):
            if FQ[t][k] == "V":
                gather("V", half("ff", k, 1024), full("ptx"), half("fu", k, 64))
        vcopy(full("hu"), full("hy"))

    def centres(t):
        return [("zin", 0, 256), ("zrr", 0, 256), ("zrr", 256, 512)][t], half("zin", t + 1)

    def natural(bank):
        for h in range(2):
            group(bank, [mm(pr(bank * 512 + 32 * k + 16 * h, 16), ("wr", h, 256, 2), half("idm", k, 16)) for k in range(8)])

    tasks("setup", 0)

    for t in range(3):
        last = t == 2
        zz = centres(t)
        expand(t)
        mine = list(zip(NETV[t], [k for k in range(8) if NETQ[t][k] == "V"]))
        for k in range(8):
            if NETQ[t][k] == "S":
                gather("S", half("net", k, 1024), full("ff"), half("hu", k, 64))
        tasks("net", t)
        ts(full("w2x"), WR, 2.0, 8.0, OP.mult, OP.min)

        slot, at = [0], {}
        steps = [(s % 2, s // 2) for s in range(16)]

        def pair():
            slot[0] += 1
            return slot[0] % 3 * 1024

        def differences(s):
            r, k = steps[s]
            o = pair()
            for c in (o, o + 512):
                group(c // 512, [mm(pr(c, 512), full("aid"), half("net", 2 * k + c // 512 % 2, 512), True, False)]
                      + [mm(pr(c + 256 * j, 256), full("nad"), zz[r], False, j == 1) for j in range(2)])
            ts(half("ind", s % 6, 1024), pr(o, 1024), MAGIC, MAGIC, OP.add, OP.is_equal)

        def counts(s):
            r, k = steps[s]
            group(6 + r, [mm(pr((6 + r) * 512 + lb * 256 + 4 * k + j, 256 - 4 * k - j, 32), sq("ind", s % 6 * 8 + 2 * j + lb), B8)
                          for j in range(4) for lb in range(2)])

        def member_sums(m):
            o = pair()
            for lb in range(2):
                group(o // 512, [mm(pr(o + 8 * lb, 8), ("mg%d" % m, 2048 * lb + b, 2048 * lb + 2048, 16), ("s8", 0, 8), b == 0, b == 15)
                                 for b in range(16)])
            ts(half("lth", m, 16), pr(o, 16), 23.5, None, OP.is_lt)

        def largest(r):
            vscan(half("cmx", r, 512), full("kmx"), pr((6 + r) * 512, 512), 0.0, OP.min, OP.max)

        def words(r):
            o = (6 + r) * 512
            group(6 + r, [mm(pr(o + 8 * lb, 8), sq("cm", lb), half("fh", 2 * r + lb, 8)) for lb in range(2)])
            tt(half("wd", r, 16), pr(o, 16), full("b16"), OP.mult)

        def lookups(r):
            o = (6 + r) * 512
            group(6 + r, [mm(pr(o, 512), full("sid"), full("eps"), True, False)]
                  + [mm(pr(o + 256 * h + a, 256 - a, 16), (oh[t + r], 2048 * h + a, 2048 * h + 2048, 16), half("wd", r, 16), False, h == 1 and a == 15)
                     for h in range(2) for a in range(16)])

        def marks(r):
            x = pr((6 + r) * 512, 512)
            ts(full("qq"), x, MAGIC, -MAGIC, OP.add, OP.add)
            tt(half("bt", r, 512), x, full("qq"), OP.is_gt)

        order = list(range(13)) + [14, 13, 15]
        top = [("cmx", 512 * r + 31, 512 * r + 512, 32) for r in range(2)]
        for n in range(16 + LAG):
            for at_step, k in mine:
                if at_step == n:
                    gather("V", half("net", k, 1024), full("ff"), half("hu", k, 64))
            if n == mine[-1][0]:
                fold(t)
            if n == 0 and t == 0:
                late_constants(1)
            for m in range(2):
                if SUMS[t][m] == n:
                    member_sums(m)
            if n < 16:
                differences(order[n])
            if n >= LAG:
                counts(order[n - LAG])
                if order[n - LAG] == 14:
                    largest(0)
                    ts(half("selh", 0, 16), top[0], 11.5, None, OP.is_lt)
                    ts(full("nsl"), top[0], 11.5, None, OP.is_ge)
                    tt(half("fh", 0, 16), half("selh", 0, 16), half("lth", 0, 16), OP.min)
            tasks(n, t)
        largest(1)
        tt(full("inn"), full("nsl"), half("lth", 1, 16), OP.min)
        ts(full("tw"), top[1], 11.5, None, OP.is_lt)
        words(0)
        tt(half("fh", 1, 16), full("tw"), full("inn"), OP.min)
        tt(half("selh", 1, 16), full("tw"), full("nsl"), OP.min)
        lookups(0)
        words(1)
        for r in range(2):
            group(r, [mm(pr(512 * r + 128 * lb, 128), half("selh", 2 * r + lb, 8), IDM, m=8) for lb in range(2)])
            act(half("st8", r), pr(512 * r, 256), parts=8)
        lookups(1)
        marks(0)
        mx, mn = half("mm", 2 * t), half("mm", 2 * t + 1)
        group(2, [mm(pr(1024, 256), full("hid"), mx, True, False), mm(pr(1024, 256), full("hid"), mn, False, False),
                  mm(pr(1024, 256), full("hid"), NH, False, True)])
        group(3, [mm(pr(1536, 8), full(n), half(b, k, 8), (n, k) == ("one", 0), (n, k) == ("mon", 3))
                  for n, b in (("one", "selh"), ("mon", "fh")) for k in range(4)])
        marks(1)
        tasks("tail", t)
        group(4, [mm(pr(2048, 256), IDM, WR, True, False)]
              + [mm(pr(2048 + 128 * (k // 2 % 2), 128), sq("bt", k), full("eid"), False, k == 7) for k in range(8)])
        ts(full("yy"), pr(1024, 256), MAGIC, -MAGIC, OP.add, OP.add)
        for r in range(2):
            group(r, [mm(pr(512 * r, 256), full("x8"), half("st8", r), k=8)])
        tt(full("w1"), pr(2048, 256), full("w2x"), OP.min)
        group(5, [mm(pr(2560, 256), full("bo"), full("w1"))])
        for r in (1, 0):
            group(2, [mm(pr(1024 + 256 * r, 256), IDM, full("yy"), True, False), mm(pr(1024 + 256 * r, 256), full("nid"), zz[r], False, True)])
        act(full("yz2"), pr(1024, 512))
        tt(("a8", 0, 8), pr(1536, 8), B8, OP.mult)
        vsum(col("sm", 2), pr(2560, 256))
        vsum(col("yat", t), ("a8", 0, 8))
        ts(col("sc"), col("sm", 2), 7168.5, 0.5, OP.is_le, OP.max)
        if not last:
            ts(full("cw"), full("cw0"), col("yat", t), 16.0, OP.add, OP.mult)
        ts(full("w2"), full("w1"), col("sc"), 128.25, OP.mult, OP.add)
        tt(half("ee", 1), pr(512, 256), half("yz2", 1), OP.mult)
        ts(WR, full("w2"), -128.0, None, OP.add)

        def centre(r):
            o = half("znew", 2 * t + r)
            group(r, [mm(pr(512 * r + 256, 256), IDM, zz[r], True, False), mm(pr(512 * r + 256, 256), full("hid"), half("ee", r), False, False),
                      mm(pr(512 * r + 256, 256), full("hid"), NH, False, True)])
            ts(o, pr(512 * r + 256, 256), MAGIC, -MAGIC, OP.add, OP.add)
            if r == 0:
                send(rank + 1 + t, ap(half("fin", t)), ap(o), "af%d" % t, [o])
            elif not last:
                send(rank - 1, ap(half("zrr", t)), ap(o), "ar%d" % (t + 1), [o])
            else:
                send(rank - 1, ap(half("fin", 3)), ap(o), "af3", [o])

        tt(half("ee", 0), pr(0, 256), half("yz2", 0), OP.mult)
        centre(1)
        natural(3)
        centre(0)
        if not last:
            act(full("wt"), pr(1536, 256))
            dmas("Y", [(T.nat[16 * k:16 * k + 1, :], ap(half("wt", k, 32))) for k in range(8)], [full("wt")], [full("nat")])
            dma("Y", ap(("yz", t * 256, t * 256 + 256)), ap(half("fin", t)), [half("fin", t)])
            tasks("post", t)

    act(full("wo"), pr(1536, 256))
    for q, ks in (("S", (0, 1, 2, 3)), ("Y", (4, 5, 6, 7))):
        dmas(q, [(T.yw[k:k + 1, :], ap(half("wo", k, 32))) for k in ks], [full("wo")])
    dma("Y", T.ya[:, :], T.yat[0:128:16, 0:3], [("yat", 0, 3)])
    dma("Y", ap(("yz", 512, 1024)), ap(("fin", 512, 1024)), [("fin", 512, 1024)])
    for s, v in totals.items():
        if known["G"].get(s, 0) < v:
            g.wait_ge(T.sem[s], v)
            known["G"][s] = v
